import numpy as np, ml_dtypes
CORES = [6,15,38,47]
N = 4
import mx_ref
BF = ml_dtypes.bfloat16
def gentries(a):
    return np.ascontiguousarray(a.reshape(8, 16, -1).transpose(0, 2, 1)).reshape(8, -1)
def gtable(e):
    e = np.asarray(e); return np.ascontiguousarray(e.reshape(8, -1, 16).transpose(0, 2, 1)).reshape(128, -1).astype(np.int32)
def gcols(t, e):
    v = np.concatenate([t.reshape(8, 16, -1, 4), np.zeros((8, 16, 1, 4), BF)], axis=2)
    return np.ascontiguousarray(np.stack([v[g][:, e[g]] for g in range(8)])).reshape(128, -1)
def tile(rs):
    return np.stack(rs, axis=2).reshape(128, -1).astype(BF)
def pick(q, e):
    c = np.concatenate([q[0].reshape(128, -1, 4), np.zeros((128, 1, 4), np.uint8)], axis=1); s = np.concatenate([q[1], np.ones((16, 1), np.uint8)], axis=1)
    return (np.ascontiguousarray(c[:, e].reshape(128, -1)), np.ascontiguousarray(s[:, e]))
def join(*qs):
    return (np.concatenate([q[0] for q in qs], axis=1), np.concatenate([q[1] for q in qs], axis=1))
def put(q, e, v):
    c, s = q[0].reshape(128, -1, 4).copy(), q[1].copy(); c[:, e] = v[0].reshape(128, -1, 4); s[:, e] = v[1]
    return (c.reshape(128, -1), s)
def pk(c, s):
    return (np.ascontiguousarray(c), mx_ref.live(s))
def emit(q):
    return q[0], q[1]
def packed(v, rng):
    q = [mx_ref.quantize(np.ascontiguousarray(v[r])) for r in range(N)]
    return np.stack([a for a, b in q]), np.stack([mx_ref.plane(b, rng) for a, b in q])
def values_of_codes():
    e, c = np.zeros((128, 128, 4), np.float32), np.zeros((128, 2, 4), np.uint8)
    e[np.arange(128), np.arange(128), 0] = 1
    c[:127, :, 0] = np.arange(256).reshape(2, 128).T[:127]
    return mx_ref.matmul(mx_ref.quantize(e.reshape(128, 512).astype(BF)), (c.reshape(128, 8), np.full((16, 2), 127, np.uint8))).T.reshape(-1).astype(np.float64)
CODE_VALUE, SCALE_VALUE = values_of_codes(), 2.0 ** (np.arange(256) - 127.0)
def decode(q):
    return (CODE_VALUE[q[0]].reshape(16, 8, -1, 4) * SCALE_VALUE[q[1]][:, None, :, None] + 0.0).reshape(128, -1).astype(np.float32)
def f(rng, *shape):
    return mx_ref.flush((rng.standard_normal(shape, dtype=np.float32) * np.exp2(rng.integers(-2, 3, shape[:-1] + (1,)))).astype(BF))
def wide(rng, *shape, cols=0):
    v = rng.standard_normal(shape, dtype=np.float32) * np.exp2(rng.integers(-12, 13, shape)).astype(np.float32)
    if cols: v *= np.repeat(np.exp2(rng.integers(-cols, cols + 1, shape[:-2] + (1, shape[-1] // 4))) * (rng.random(shape[:-2] + (1, shape[-1] // 4)) > 0.0625), 4, axis=-1).astype(np.float32)
    return mx_ref.flush(v.astype(BF))
C, K, M, R = 448, 32, 14, 3
BASE = M * np.concatenate([np.arange(K), np.arange(K)])
def matrices(a):
    return a.reshape(8, 16, K // 16, M, M).transpose(0, 2, 1, 3, 4).reshape(8, K, M, M).astype(np.int64)
def stored(m):
    return np.ascontiguousarray(m.reshape(8, K // 16, 16, M, M).transpose(0, 2, 1, 3, 4)).reshape(128, -1)
def numbers_of(rng):
    return {"x": np.array(f(rng, N, 128, 4 * C)), "u": np.array(f(rng, N, 128, 512)), "v": np.array(f(rng, N, 128, 512))}
def nodes(rng):
    return np.stack([gtable(np.stack([rng.permutation(C) for g in range(8)])) for r in range(N)])
def arrows(a):
    a = np.triu(a, 1)
    a = a - a.swapaxes(-1, -2)
    return np.stack([stored(a[r]) for r in range(N)]).astype(np.int32)
def some_arrows(rng):
    return rng.integers(-3, 4, (N, 8, K, M, M)) * (rng.random((N, 8, K, M, M)) < 0.6)
def laid(w, nd):
    w = w.reshape(N, 8, 16, C, 4)
    t = np.zeros_like(w)
    for r in range(N):
        e = gentries(nd[r])
        for g in range(8): t[r, g][:, e[g]] = w[r, g]
    return t.reshape(N, 128, 4 * C).astype(BF)
def weights(rng, still=[], by=1.0):
    w = np.array(f(rng, N, 128, 2048)).reshape(N, 8, 16, 4, 8, 16, 4)
    for i in still:
        w[:, :, i] = 0
        w[:, :, :, :, :, i] = 0
    w = mx_ref.flush((w.astype(np.float32) * np.float32(by)).astype(BF))
    c, s = packed(np.ascontiguousarray(w).reshape(N, 128, 2048), rng)
    return {"wc": c, "ws": s}
def setup_inputs(rng):
    return {**numbers_of(rng), "nd": nodes(rng), "ar": arrows(some_arrows(rng)), **weights(rng)}
def setup_inputs_ties(rng):
    d = numbers_of(rng)
    nd = nodes(rng)
    w = d["x"].reshape(N, 8, 16, C, 4)
    w[:, :, 0] = 0
    w[:, :, 0, :, 0] = rng.integers(1, 4, (N, 8, C)).astype(np.float32).astype(BF)
    u = d["u"].reshape(N, 128, 128, 4)
    u[:, :, ::16] = 0
    o = rng.permutation(N)
    for r in range(N):
        for h in range(0, 128, 16): u[r, h, h, 0] = 0.0 if r == o[0] else -1.0 if r == o[1] else 1.0
    return {"x": laid(w, nd), "u": u.reshape(N, 128, 512), "v": d["v"], "nd": nd, "ar": arrows(some_arrows(rng)), **weights(rng, [0])}
def setup_inputs_near(rng):
    d = numbers_of(rng)
    nd = nodes(rng)
    w = d["x"].astype(np.float32).reshape(N, 8, 16, K, M, 4)
    w[:, :, 0] = 0
    w[:, :, 8:] = 0
    s = rng.integers(0, 16, (N, 8, K, M))
    w[:, :, 8] = ((s[..., None] >> np.arange(4)) & 1) * np.exp2(np.arange(4) - 23.0)
    u = d["u"].reshape(N, 128, 128, 4)
    u[:, :, ::16] = 0
    o = rng.permutation(N) % 4
    for r in range(N):
        k = 1.0 if o[r] == 0 else 2.0 ** -30
        c = rng.choice([-1.0, 1.0], (8, K, 1))
        if o[r] < 2:
            w[r, :, 0, :, :, 0] = c
            w[r, :, 11, :, :, 0] = 2.0 ** -10
        elif o[r] == 2:
            far = np.argsort(rng.random((8, K, M)), axis=2)
            w[r, :, 0, :, :, 0] = 1.0 * (far == 0) - 1.0 * (far == 1)
            for g in rng.permutation(8)[:4]: w[r, g, 0, rng.integers(K), rng.integers(M), 0] = 2.0 ** 26
        else:
            w[r, :, 8] = 0
            w[r, :, 8, :, :, 0] = c * rng.integers(8, 16, (8, K, M)) * 2.0 ** -27
        for h in range(0, 128, 16):
            if o[r] < 2:
                u[r, h, h, 0] = k
                u[r, h + 11, h, 0] = k
            if o[r] == 2: u[r, h, h, 0] = 16.0
            if o[r] < 3: u[r, h + 8, h] = k
            else: u[r, h + 8, h, 0] = k
    return {"x": laid(w, nd), "u": u.reshape(N, 128, 512), "v": d["v"], "nd": nd, "ar": arrows(some_arrows(rng)), **weights(rng, [0, 8, 9, 10, 11, 12, 13, 14, 15])}
def setup_inputs_huge(rng):
    d = numbers_of(rng)
    o = rng.permutation(N)
    a = some_arrows(rng)
    x = 0.8 + 0.1 * rng.random((N, 128, C, 4))
    u = d["u"].reshape(N, 128, 128, 4)
    for r in range(N):
        c = rng.choice([-1.0, 1.0], (C, 1))
        k = 2.0 ** 30 * (1.0 - 0.1 * rng.random((128, 8, 4)))
        if o[r] < 2: c = -np.ones((C, 1))
        if o[r] == 3:
            c = -np.ones((C, 1))
            c[rng.permutation(C)[:K]] = 1.0
            x[r] = 0.9375
            k[:] = 2.0 ** 30
        if o[r] % 2 == 1: a[r] = 0
        x[r] *= c * (2.0 ** 30 if o[r] % 2 == 1 else 2.0 ** 28 if o[r] == 0 else 2.0 ** 27)
        u[r, :, ::16] = k.astype(np.float32).astype(BF)
    return {"x": x.astype(np.float32).reshape(N, 128, 4 * C).astype(BF), "u": u.reshape(N, 128, 512), "v": d["v"], "nd": nodes(rng), "ar": arrows(a), **weights(rng, [], 2.0 ** -14)}
def setup_inputs_knots(rng):
    d = numbers_of(rng)
    e = rng.permutation(N)
    kind = rng.integers(0, 4, (N, 8, K, 1, 1))
    kind[e[0]] = 0
    kind[e[1]] = 1
    sign = rng.choice([-1, 1], (N, 8, K, M, M))
    half = sign * (rng.random((N, 8, K, M, M)) < 0.5)
    a = np.where(kind == 0, 0, np.where(kind == 1, sign * rng.integers(1, 4, (N, 8, K, M, M)), np.where(kind == 2, half, 3 * half)))
    place = np.arange(8)[:, None, None] * 4 + np.arange(4)
    most = place == rng.integers(0, 32, (N, 16, 1, C, 1))
    x = (129.0 + 2.0 * rng.integers(0, 64, (N, 16, 8, C, 4))) * np.exp2(-7.0 - rng.integers(8, 15, (N, 16, 8, C, 4)))
    x = np.where(most, 1.96875, x) * rng.choice([-1.0, 1.0], (N, 16, 8, C, 4)) * np.exp2(rng.integers(-2, 3, (N, 16, 1, C, 1)))
    return {"x": x.astype(np.float32).reshape(N, 128, 4 * C).astype(BF), "u": d["u"], "v": d["v"], "nd": nodes(rng), "ar": arrows(a), **weights(rng)}
def setup_inputs_spread(rng):
    d = setup_inputs(rng)
    d["x"] = wide(rng, N, 128, 4 * C, cols=6)
    return d
def check_inputs(d):
    b = []
    for k in ("x", "u", "v"):
        a = np.abs(d[k].astype(np.float32))
        if not (np.isfinite(a).all() and ((a == 0) | (a >= 2.0 ** -30) & (a <= 2.0 ** 30)).all()): b.append("a value of " + k)
    none, least, most = [emit(mx_ref.quantize(np.full((128, 16), k, np.float32).astype(BF)))[1][0, 0] for k in (0.0, 2.0 ** -30, 2.0 ** 30)]
    for r in range(N):
        if (np.sort(gentries(d["nd"][r]), axis=1) != np.arange(C)).any(): b.append("nd: a group without every column once")
        a = matrices(d["ar"][r])
        if (np.abs(a) > 3).any(): b.append("an entry of ar")
        if (a != -a.swapaxes(-1, -2)).any(): b.append("ar: B[j, i] isn't -B[i, j]")
        if ((d["wc"][r] & 0x7F) == 0x7F).any(): b.append("wc: a code that is no number")
        s = mx_ref.live(d["ws"][r])
        if ((s != none) & ((s < least) | (s > most))).any(): b.append("ws: a scale out of range")
    return b
def parts(t, n, e):
    return gcols(t, np.where(e < 0, -1, np.take_along_axis(n, BASE + np.maximum(e, 0), axis=1))).astype(np.float32)
def pair(t, n, w):
    e = np.argsort(-w, axis=2, kind="stable")[:, :, :2]
    e = np.where(np.take_along_axis(w, e, axis=2) > 0, e, -1)
    return ((parts(t, n, e[:, :, 0]) + parts(t, n, e[:, :, 1])) * np.float32(0.5)).astype(BF).astype(np.float32)
def reference(x, u, v, nd, ar, wc, ws):
    qu = [mx_ref.quantize(u[r]) for r in range(N)]
    lay = [pk(wc[r], ws[r]) for r in range(N)]
    now = [x[r] for r in range(N)]
    node = [gentries(nd[r]) for r in range(N)]
    arrow = [matrices(ar[r]) for r in range(N)]
    for t in range(R):
        held, made, sent, into = [], [], [], []
        for r in range(N):
            q = mx_ref.quantize(now[r])
            own = decode(q).astype(BF)
            s = mx_ref.matmul(qu[r], q)[::16] + np.float32(0.0)
            s = np.take_along_axis(s, node[r], axis=1).reshape(8, K, M)
            first = np.argmax(s, axis=2)
            row = np.take_along_axis(arrow[r], first[:, :, None, None], axis=2)[:, :, 0]
            free = (row == 0) & (np.arange(M) != first[:, :, None])
            second = np.argmax(np.where(free, s, -np.inf), axis=2)
            k = np.concatenate([first, second], axis=1)
            full = np.concatenate([np.ones((8, K), bool), free.any(axis=2)], axis=1)
            row = np.concatenate([row, np.take_along_axis(arrow[r], second[:, :, None, None], axis=2)[:, :, 0]], axis=1) * full[:, :, None]
            y = (np.maximum(pair(own, node[r], -row), pair(own, node[r], row)) - parts(own, node[r], np.where(full, k, -1))).astype(BF)
            held.append(own)
            made.append(y)
            sent.append(mx_ref.quantize(y))
            e = np.tile(np.arange(C), (8, 1))
            g, i = np.nonzero(full)
            e[g, np.take_along_axis(node[r], BASE + k, axis=1)[g, i]] = C + i
            into.append(e)
            more = (np.abs(row)[:, :, :, None] * row[:, :, None, :] - row[:, :, :, None] * np.abs(row)[:, :, None, :]) // 2
            turn = np.ones((8, 2 * K, M), np.int64)
            np.put_along_axis(turn, k[:, :, None], np.where(full, -1, 1)[:, :, None], axis=2)
            turn = turn[:, :K] * turn[:, K:]
            arrow[r] = np.clip(arrow[r] + more[:, :K] + more[:, K:], -3, 3) * turn[:, :, :, None] * turn[:, :, None, :]
        for r in range(N):
            q = sent[(r - 1) % N]
            new = tile([mx_ref.matmul(pick(lay[r], np.arange(128 * b, 128 * b + 128)), q) * np.float32(0.03125) + made[r][:, b::4].astype(np.float32) for b in range(4)])
            now[r] = gcols(np.concatenate([held[r], new], axis=1), into[r])
    y, oa = np.zeros((N, 128, C), np.float32), np.zeros(ar.shape, np.float32)
    oc, osc = np.zeros((N, 128, 4 * C), np.uint8), np.zeros((N, 16, C), np.uint8)
    for r in range(N):
        q = mx_ref.quantize(now[r])
        y[r] = mx_ref.matmul(mx_ref.quantize(v[r]), q)
        oa[r] = stored(arrow[r])
        oc[r], osc[r] = emit(q)
    return {"y": y, "oa": oa, "oc": oc, "osc": osc}

@@ -1,0 +1,434 @@
+from concourse.mybir import dt, AluOpType, ActivationFunctionType
+
+ROUNDS, C = 3, 448
+XW = 1936
+UNIT = 65536.0
+MARK = 16384.0
+FLOOR = 65536.0 + 4 * 448
+BIG = 2.0 ** 99
+LOW = -(2.0 ** 98)
+RND16 = 1.5 * 2.0 ** 39
+RND0 = 1.5 * 2.0 ** 23
+
+F32, B16, I32, U16, QC, U8 = "float32", "bfloat16", "int32", "uint16", "float8_e4m3fn_x4", "uint8"
+SCRATCH = {"pp": ("psum", [128, 1024], F32), "pd": ("psum", [128, 2048], F32), "pq": ("psum", [128, 1024], F32)}
+for _d, _list in [
+        (B16, "xin 1792 ft0 1936 ft1 1936 ft2 1936 ut 512 vt 512 eb 516 ones 516 ie 512 mask 448 rst16 448 rst14 28 sg 1344 "
+              "cw 528 ds0 1024 ds1 1024 ds2 1024 av 160 eq 56 ph0 28 xg 896 st 1344 so 1344 ltb 56 cnt 56 ge 512 rf 1024 "
+              "ag 512 su2 512 ys 512 yd 512 yt 512 y32 256 vv 256"),
+        (F32, "iw 448 r1 448 r2 448 r3 448 ps 448 smk 448 scn 448 oa1 400 wb 256 yo 448 key 113 ep 112 tmn 112 p2 112 capz 112"),
+        (I32, "ndin 28 arin 392")]:
+    _w = _list.split()
+    for _k in range(0, len(_w), 2):
+        SCRATCH[_w[_k]] = ("sbuf", [128, int(_w[_k + 1])], _d)
+for _n, _c in [("qw", 512), ("qu", 128), ("qr", 128), ("qv", 128), ("qe", 512), ("qx0", 448), ("qx1", 448), ("qx2", 448),
+               ("qx3", 448), ("qy0", 128), ("qy1", 128), ("qy2", 128), ("ld0", 128), ("ld1", 128), ("ld2", 128)]:
+    SCRATCH[_n] = ("sbuf", [128, _c], QC)
+    SCRATCH["s" + _n] = ("sbuf", [128, _c], U8)
+SMALL = {}
+for _buf, _d, _step, _list in [
+        ("smalli", I32, 8, "lane0 56 lane 56 t28a 28 t28b 28 t28c 28 t8 8 ndw 32 ndh 32 ndl 32 dum 2 dum0 2 kc 28 h14 14 d14 14 "
+                           "h196 14 t14a 14 t14b 14 t14c 14 t14d 14 t14e 14 t14f 14 fj 56 fh 56 fi0 56 fi 56 fl 56 "
+                           "fm 56 fn 56 fo 56 f1 56 f2 56 f3 56 f4 56 f5 56 f6 56 f7 56 f8 56 f9 56 fa 56 fx 8 lfi 64 oe0 25 oi 16 "
+                           "oim 16 ow 4"),
+        ("smallu", U16, 16, "lrep 28 lu 8 ndn 28 nd16 28 li 14 lk 14 lc 14 lf 64 loa 25 off 64 ox 16"),
+        ("smallf", F32, 8, "lanef 1 capa 28 capb 30 nd4 28 kb 28 oe 25 o1 25 o2 25 o3 25 o4 25 pm0 28 pm1 30 pen 28 s2 30")]:
+    _w, _at = _list.split(), 0
+    for _k in range(0, len(_w), 2):
+        SMALL[_w[_k]] = (_buf, _at, int(_w[_k + 1]))
+        _at += (int(_w[_k + 1]) + _step - 1) // _step * _step
+    SCRATCH[_buf] = ("sbuf", [128, _at], _d)
+
+NDMA = 24
+SEMAPHORES = ["cv", "cs", "ct", "cg", "ready", "loc", "arr0", "arr1", "arr2"] + ["dma%d" % _k for _k in range(NDMA)]
+
+
+def rank_program(g, core, T, topo):
+    rank = T.rank_of(core)
+    if rank is None:
+        return
+    A = AluOpType
+    COPY = ActivationFunctionType.Copy
+    n = len(T.cores)
+    nxt, prv = T.cores[(rank + 1) % n], T.cores[(rank - 1) % n]
+
+    queue = {"v": g.vector, "s": g.scalar, "t": g.tensor, "g": g, "y": g.sync}
+    semof = {"v": "cv", "s": "cs", "t": "ct", "g": "cg"}
+    count = {"cv": 0, "cs": 0, "ct": 0, "cg": 0}
+    state, seen, ndma = {}, {}, [0]
+
+    def entry(t):
+        return state.setdefault(t, [[], [], [], True])
+
+    def need(q, sem, val):
+        if seen.get((q, sem), 0) < val:
+            queue[q].wait_ge(T.sem[sem], val)
+            seen[(q, sem)] = val
+
+    def order(q, R, W, dma):
+        want = []
+        for t in R:
+            want += entry(t)[0]
+        for t in W:
+            s = entry(t.lstrip("+"))
+            if t[0] != "+" or s[1] or s[3]:
+                s[2] = s[0] + [e for e in s[1] if dma or e[2] != q]
+                s[0], s[1], s[3] = [], [], t[0] != "+"
+            want += s[2]
+        most = {}
+        for sem, val, w in want:
+            most[sem] = max(most.get(sem, 0), val)
+        for sem in most:
+            need(q, sem, most[sem])
+
+    def note(R, W, e):
+        for t in R:
+            entry(t)[1].append(e)
+        for t in W:
+            entry(t.lstrip("+"))[0].append(e)
+
+    def op(q, R, W, f):
+        R, W = R.split(), W.split()
+        order(q, R, W, False)
+        s = semof[q]
+        count[s] += 1
+        f(queue[q]).then_inc(T.sem[s], 1)
+        note(R, W, (s, count[s], q))
+
+    def dma(q, R, W, out, in_):
+        R, W = R.split(), W.split()
+        order(q, R, W, True)
+        s = "dma%d" % ndma[0]
+        ndma[0] += 1
+        queue[q].dma_start(out, in_).then_inc(T.sem[s], 16)
+        note(R, W, (s, 16, "dma"))
+
+    def b(name, lo=0, hi=None, step=1):
+        buf, at, cols = SMALL[name] if name in SMALL else (name, 0, SCRATCH[name][1][1])
+        hi = cols if hi is None else hi
+        return T[buf][:, at + lo:at + hi:step] if step > 1 else T[buf][:, at + lo:at + hi]
+
+    def ts(R, W, out, in0, s1, op0, s2=None, op1=None):
+        if op1 is None:
+            op("v", R, W, lambda e: e.tensor_scalar(out, in0, s1, None, op0))
+        else:
+            op("v", R, W, lambda e: e.tensor_scalar(out, in0, s1, s2, op0, op1))
+
+    def tt(R, W, out, in0, in1, o):
+        op("v", R, W, lambda e: e.tensor_tensor(out, in0, in1, o))
+
+    def cp(R, W, out, in_):
+        op("v", R, W, lambda e: e.tensor_copy(out, in_))
+
+    def fill(W, out, c):
+        op("v", "", W, lambda e: e.memset(out, c))
+
+    def scan(R, W, out, d0, d1, init, o0, o1):
+        op("v", R, W, lambda e: e.tensor_tensor_scan(out, d0, d1, init, o0, o1))
+
+    def act(R, W, out, in_, scale=1.0):
+        if scale == 1.0:
+            op("s", R, W, lambda e: e.activation(out, in_, COPY))
+        else:
+            op("s", R, W, lambda e: e.activation(out, in_, COPY, scale=scale))
+
+    def quant(R, W, q, s, in_):
+        op("v", R, W, lambda e: e.quantize_mx(q, s, in_))
+
+    def mm(R, W, out, a, sa, m, sm):
+        op("t", R, W, lambda e: e.matmul_mx(out, a, sa, m, sm, True, True))
+
+    def iota(W, out, pattern, base, cm, small=False):
+        if small:
+            op("g", "", W, lambda e: e.iota(out, pattern, base, cm, allow_small_or_imprecise_dtypes=True))
+        else:
+            op("g", "", W, lambda e: e.iota(out, pattern, base, cm))
+
+    dma("y", "", "ndin", b("ndin"), T.nd[:, :])
+    dma("s", "", "xb", b("xin", 896, 1792), T.x[:, 896:1792])
+    dma("y", "", "ut", b("ut"), T.u[:, :])
+    dma("y", "", "xa", b("xin", 0, 896), T.x[:, 0:896])
+    dma("y", "", "arin", b("arin"), T.ar[:, :])
+    dma("y", "", "sw", b("sqw"), T.ws[:, :])
+    dma("y", "", "qw", T.qw[:, :].bitcast(dt.uint8), T.wc[:, :])
+    dma("y", "", "vt", b("vt"), T.v[:, :])
+
+    iota("lane0", b("lane0"), [[0, 56]], 0, 1)
+    iota("t28a", b("t28a"), [[224, 2], [1, 14]], 0, 0)
+    iota("iw", b("iw"), [[1, 448]], 0, 0, True)
+    iota("t8", b("t8"), [[16, 8]], 0, 0)
+    iota("ie", b("ie"), [[0, 32], [1, 16]], 0, 0, True)
+    fill("yt", b("yt"), 0.0)
+    for t in range(ROUNDS):
+        quant("yt", "ld%d" % t, b("ld%d" % t), b("sld%d" % t), b("yt"))
+    fill("ones", b("ones"), 1.0)
+    ts("lane0", "lane", b("lane"), b("lane0"), 15, A.bitwise_and)
+    fill("capa", b("capa"), BIG)
+    fill("capb", b("capb"), BIG)
+    ts("lane", "t28b", b("t28b"), b("lane", 0, 28), 14, A.mult)
+    cp("lane", "lanef", b("lanef"), b("lane", 0, 1))
+    fill("rst14", b("rst14"), 1.0)
+    tt("t28b t28a", "t28c", b("t28c"), b("t28b"), b("t28a"), A.add)
+    fill("capz", b("capz"), BIG)
+    fill("key0", b("key", 0, 1), 0.0)
+    cp("t28c", "lrep", b("lrep"), b("t28c"))
+    fill("cwk", b("cw", 512, 528), 0.0)
+    fill("ndw", b("ndw"), 0)
+    fill("s2z", b("s2"), LOW)
+    cp("ndin", "ndn", b("ndn"), b("ndin"))
+    act("iw ndn", "r1", b("r1"), T.iw[:, 0:448].indirect(b("ndn")))
+    cp("t8", "lu", b("lu"), b("t8"))
+    fill("capa", b("capa", 0, 28, 14), -BIG)
+    fill("capb", b("capb", 0, 30, 15), -BIG)
+    fill("rst14", b("rst14", 0, 28, 14), 0.0)
+    fill("capz", b("capz", 0, 112, 14), FLOOR)
+    fill("cwk", b("cw", 512, 513), MARK)
+    for t in range(ROUNDS):
+        fill("fz%d" % t, b("ft%d" % t, 1792, XW), 0.0)
+    ts("ie lanef", "mask", b("mask"), b("ie", 0, 448), b("lanef"), A.is_equal)
+    ts("ie", "rst16", b("rst16"), b("ie", 0, 448), 0.0, A.not_equal)
+
+    iota("h14", b("h14"), [[14, 2], [0, 7]], 0, 0)
+    iota("d14", b("d14"), [[0, 2], [1, 7]], 1, 0)
+    mask = topo.mask(core, prv)
+    rid, pid = topo.addr(prv)[:2]
+    order("g", ["ld0", "ld1", "ld2"], [], False)
+    g.remote_sem_update(T.sem["ready"], T.sem["loc"], pid, rid, mask)
+    nloc = [len(topo.engines(core, prv))]
+    op("g", "ones", "eb", lambda e: e.affine_select(b("eb"), b("ones"), [[-1, 516]], A.is_equal, 0.0, 3, 4))
+    iota("dum0", b("dum0"), [[16, 2]], 449, 0)
+    iota("fj", b("fj"), [[0, 2], [1, 14], [0, 2]], 0, 0)
+    iota("fi0", b("fi0"), [[0, 28], [8, 2]], 0, 0)
+    iota("h196", b("h196"), [[196, 2], [0, 7]], 0, 0)
+    iota("fh", b("fh"), [[112, 2], [0, 28]], 0, 0)
+    iota("+fx", b("fx", 0, 4), [[32, 2], [8, 2]], 448, 0)
+    iota("+fx", b("fx", 4, 8), [[32, 2], [8, 2]], 464, 0)
+    iota("kc", b("kc"), [[0, 2], [-2048, 14]], 14 * 2048, 0)
+    iota("ds0", b("ds0"), [[0, 512], [-1, 2]], 0, 0, True)
+    iota("yc", b("so", 0, 512), [[0, 256], [1, 2]], 0, 0, True) if False else None
+    iota("yd", b("yd"), [[0, 256], [1, 2]], 0, 0, True)
+    iota("oe0", b("oe0"), [[16, 25]], 0, 0)
+    for s, c in ((0, 0), (3, 1), (4, -1), (5, 1)):
+        iota("+sgc", b("sg", s, 1344, 6), [[0, 224]], c, 0, True)
+    iota("st1", b("st", 1, 1344, 6), [[0, 224]], 0, 0, True)
+
+    quant("ut", "qu", b("qu"), b("squ"), b("ut"))
+    op("v", "qu lu", "qr", lambda e: e.tensor_copy(T.qr[:, 0:128].bitcast(dt.uint32), T.qu[:, 0:128].bitcast(dt.uint32).indirect(b("lu"))))
+    act("qu lu", "sr", b("sqr"), T.squ[:, 0:128].indirect(b("lu")))
+    tt("r1 lrep mask", "r2", b("r2"), T.r1[:, 0:448].indirect(b("lrep")), b("mask"), A.mult)
+    scan("rst16 r2", "r3", b("r3"), b("rst16"), b("r2"), 0.0, A.mult, A.add)
+    for k in range(4):
+        quant("eb", "+qe", T.qe[:, 128 * k:128 * k + 128], T.sqe[:, 128 * k:128 * k + 128], T.eb[:, 3 - k:515 - k])
+    cp("r3", "nd16", b("nd16"), b("r3", 15, 448, 16))
+
+    def quantise_state(r, src, ta, tb):
+        qx, sx = T["qx%d" % r], T["sqx%d" % r]
+        quant(ta, "qa%d" % r, qx[:, 0:224], sx[:, 0:224], src[:, 0:896])
+        quant(tb, "qb%d" % r, qx[:, 224:448], sx[:, 224:448], src[:, 896:1792])
+        return qx, sx
+
+    def begin(r, src, ta, tb):
+        ft = "ft%d" % r
+        qx, sx = quantise_state(r, src, ta, tb)
+        mm("qr sr qa%d" % r, "pp0", T.pp[:, 0:224], b("qr"), b("sqr"), qx[:, 0:224], sx[:, 0:224])
+        mm("qr sr qb%d" % r, "pp1", T.pp[:, 512:736], b("qr"), b("sqr"), qx[:, 224:448], sx[:, 224:448])
+        for k in range(4):
+            mm("qe qa%d qb%d" % (r, r), "pd%d" % k, T.pd[:, 512 * k:512 * k + 448], T.qe[:, 128 * k:128 * k + 128],
+               T.sqe[:, 128 * k:128 * k + 128], qx[:, 0:448], sx[:, 0:448])
+        act("pp0", "ps0", b("ps", 0, 224), T.pp[:, 0:224])
+        for k in range(4):
+            act("pd%d" % k, "+" + ft, b(ft, k, 1792, 4), T.pd[:, 512 * k:512 * k + 448])
+
+    begin(0, T.xin, "xa", "xb")
+    tt("d14 lane", "t14a", b("t14a"), b("d14"), b("lane", 0, 14), A.add)
+    ts("lane", "fm", b("fm"), b("lane"), 1, A.arith_shift_right)
+    ts("lane", "fn", b("fn"), b("lane"), 1, A.bitwise_and)
+    tt("dum0 lane", "dum", b("dum"), b("dum0"), b("lane", 0, 2), A.add)
+    ts("t14a", "t14b", b("t14b"), b("t14a"), 14, A.is_ge, -14, A.mult)
+    tt("fm fn", "fo", b("fo"), b("fm"), b("fn"), A.subtract)
+    for h in range(2):
+        cp("r3", "+ndw", b("ndw", 16 * h, 16 * h + 14), b("r3", 224 * h + 15, 224 * h + 224, 16))
+    cp("dum", "+ndw", b("ndw", 14, 32, 16), b("dum"))
+    ts("lane", "t14e", b("t14e"), b("lane", 0, 14), 14, A.mult)
+    ts("fo", "fl", b("fl"), b("fo"), 1, A.add)
+    tt("t14a t14b", "t14c", b("t14c"), b("t14a"), b("t14b"), A.add)
+    ts("ndw", "ndh", b("ndh"), b("ndw"), 4, A.arith_shift_right)
+    ts("ndw", "ndl", b("ndl"), b("ndw"), 15, A.bitwise_and)
+    tt("fl fi0", "fi", b("fi"), b("fl"), b("fi0"), A.add)
+    tt("t14e h196", "t14f", b("t14f"), b("t14e"), b("h196"), A.add)
+    tt("t14c h14", "t14d", b("t14d"), b("t14c"), b("h14"), A.add)
+    tt("fi fj", "f1", b("f1"), b("fi"), b("fj"), A.subtract)
+    tt("t14f t14c", "t14g", b("t14a"), b("t14f"), b("t14c"), A.add)
+    cp("t14d", "lk", b("lk"), b("t14d"))
+    ts("f1", "f2", b("f2"), b("f1"), 0, A.is_lt, 14, A.mult)
+    ts("t14g", "t14h", b("t14b"), b("t14a"), 391, A.min)
+    ts("ndh", "+cwn", b("cw", 448, 480), b("ndh"), 64, A.mult)
+    tt("f1 f2", "f3", b("f3"), b("f1"), b("f2"), A.add)
+    cp("t14h", "lc", b("lc"), b("t14b"))
+    ts("ndl", "+cwn", b("cw", 480, 512), b("ndl"), 4, A.mult)
+    ts("f3", "f4", b("f4"), b("f3"), 16, A.mult, -16, A.add)
+    ts("f3", "f6", b("f6"), b("f3"), -16, A.mult, 432, A.add)
+    ts("f3", "f8", b("f8"), b("f3"), 7, A.is_le)
+    tt("f4 fj", "f5", b("f5"), b("f4"), b("fj"), A.add)
+    tt("f6 fi", "f7", b("f7"), b("f6"), b("fi"), A.add)
+    ts("arin lc", "cst", b("st", 0, 1344, 6), T.arin[:, 0:392].indirect(b("lc")), UNIT, A.mult)
+    tt("f5 f7", "f9", b("f9"), b("f5"), b("f7"), A.subtract)
+    ts("f3", "f4", b("f4"), b("f3"), 0, A.is_equal, 512, A.mult)
+    tt("f8 f9", "fa", b("fa"), b("f8"), b("f9"), A.mult)
+    ts("fi", "f6", b("f6"), b("fi"), 14, A.is_ge, 513, A.mult)
+    tt("fa f7", "f1", b("f1"), b("fa"), b("f7"), A.add)
+    tt("fx fl", "+lfi", b("lfi", 0, 4), b("fx", 0, 4), b("fl", 0, 4), A.add)
+    tt("f1 fh", "f2", b("f2"), b("f1"), b("fh"), A.add)
+    tt("fx fl", "+lfi", b("lfi", 60, 64), b("fx", 4, 8), b("fl", 0, 4), A.add)
+    tt("f2 f4", "f5", b("f5"), b("f2"), b("f4"), A.max)
+    ts("r3", "nd4", b("nd4"), b("r3", 15, 448, 16), 4.0, A.mult)
+    tt("f5 f6", "+lfi", b("lfi", 4, 60), b("f5"), b("f6"), A.max)
+    tt("nd4 kc", "kb", b("kb"), b("nd4"), b("kc"), A.add)
+    cp("lfi", "lf", b("lf"), b("lfi"))
+
+    def lay_out():
+        act("cst", "cw0", b("cw", 0, 224), b("st", 0, 1344, 6))
+        act("cst", "cw1", b("cw", 224, 448), b("st", 0, 1344, 6), -1.0)
+        act("cw0 cw1 cwk cwn lf", "ds1", b("ds1"), T.cw[:, 0:528].indirect(b("lf")))
+
+    lay_out()
+
+    def make_arrow_constants():
+        tt("h14 lane", "t14d", b("t14d"), b("h14"), b("lane", 0, 14), A.add)
+        fill("av0 av1 av2", b("av"), 0.0)
+        cp("t14d", "li", b("li"), b("t14d"))
+
+    def choose(k, pm, wide):
+        o = 28 * k
+        for h in range(2):
+            ts(pm, "+lt%d" % k, b("ltb", o + 14 * h, o + 14 * h + 14), b(pm, wide * h, wide * h + 14), b(pm, wide * h + wide - 1, wide * h + wide), A.is_lt)
+        scan("rst14 lt%d" % k, "cnt%d" % k, b("cnt", o, o + 28), b("rst14"), b("ltb", o, o + 28), 0.0, A.mult, A.add)
+        for h in range(2):
+            ts("ie cnt%d" % k, "+ge", b("ge", 256 * h, 256 * h + 256), b("ie", 256 * h, 256 * h + 256), b("cnt", o + 14 * h + 13, o + 14 * h + 14), A.is_gt)
+        scan("ge ds2", "rf%d" % k, b("rf", 512 * k, 512 * k + 512), b("ge"), b("ds2", 1, 1024, 2), 0.0, A.mult, A.add)
+
+    def rows(k):
+        return b("rf", 512 * k + 46, 512 * k + 46 + 28 * 16 - 15, 16)
+
+    def differences():
+        scan("ds0 ds1", "ds2", b("ds2"), b("ds0"), b("ds1"), 0.0, A.mult, A.add)
+
+    rid, pid = topo.addr(nxt)[:2]
+    mask = topo.mask(core, nxt)
+    engines = len(topo.engines(core, nxt))
+
+    for r in range(ROUNDS):
+        ft, fz = "ft%d" % r, "ft%d fz%d" % (r, r)
+        if r:
+            begin(r, T["ft%d" % (r - 1)], "ft%d" % (r - 1), "ft%d" % (r - 1))
+            differences()
+        cp("pp1", "ps1", b("ps", 224, 448), T.pp[:, 512:736])
+        tt("ps0 ps1 nd16 mask", "smk", b("smk"), T.ps[:, 0:448].indirect(b("nd16")), b("mask"), A.mult)
+        scan("rst16 smk", "scn", b("scn"), b("rst16"), b("smk"), 0.0, A.mult, A.add)
+        scan("capa scn", "pm0", b("pm0"), b("capa"), b("scn", 15, 448, 16), 0.0, A.min, A.max)
+        if r == 0:
+            differences()
+        choose(0, "pm0", 14)
+        ts("rf0", "pen", b("pen"), rows(0), 0.0, A.not_equal, -BIG, A.mult)
+        tt("kb rf0", "+key", b("key", 1, 29), b("kb"), rows(0), A.add)
+        for h in range(2):
+            tt("scn pen s2z", "+s2", b("s2", 15 * h, 15 * h + 14), b("scn", 224 * h + 15, 224 * h + 224, 16), b("pen", 14 * h, 14 * h + 14), A.add)
+        tt("kb rf0", "+key", b("key", 57, 85), b("kb"), rows(0), A.subtract)
+        scan("capb s2 s2z", "pm1", b("pm1"), b("capb"), b("s2"), 0.0, A.min, A.max)
+        tt("rf0", "+ow", b("ow", 0, 2), b("rf", 14, 495, 480), b("rf", 30, 511, 480), A.add)
+        choose(1, "pm1", 15)
+        tt("rf1", "+ow", b("ow", 2, 4), b("rf", 526, 1007, 480), b("rf", 542, 1023, 480), A.add)
+        tt("kb rf1", "+key", b("key", 29, 57), b("kb"), rows(1), A.add)
+        tt("kb rf1", "+key", b("key", 85, 113), b("kb"), rows(1), A.subtract)
+        for t in range(4):
+            ts("ow", "+ox", b("ox", 4 * t, 4 * t + 4), b("ow"), t, A.add)
+        scan("key key0 capz", "ep", b("ep"), b("key", 0, 112), b("capz"), BIG, A.max, A.min)
+        for t in range(4):
+            act(fz + " ox", "+own", b("ys", 2 * t + 1, 512, 8), T[ft][:, 0:XW].indirect(b("ox", 4 * t, 4 * t + 4)), -2.0)
+        tt("ep key", "tmn", b("tmn"), b("ep"), b("key", 1, 113), A.min)
+        tt("ep key", "+oi", b("oi", 0, 8), b("ep", 13, 112, 14), b("key", 14, 113, 14), A.max)
+        scan("capz tmn", "p2", b("p2"), b("capz"), b("tmn"), FLOOR, A.min, A.max)
+        cp("p2", "+oi", b("oi", 8, 16), b("p2", 13, 112, 14))
+        ts("oi", "oim", b("oim"), b("oi"), 2047, A.bitwise_and)
+        for t in range(4):
+            ts("oim", "off%d" % t, b("off", 16 * t, 16 * t + 16), b("oim"), t, A.add)
+        for t in range(4):
+            act(fz + " off%d" % t, "ag%d" % t, b("ag", t, 512, 4), T[ft][:, 0:XW].indirect(b("off", 16 * t, 16 * t + 8)))
+        for t in range(4):
+            tt(fz + " off%d ag%d" % (t, t), "+su", b("su2", t, 512, 4), T[ft][:, 0:XW].indirect(b("off", 16 * t + 8, 16 * t + 16)), b("ag", t, 512, 4), A.add)
+        tt("su", "mm", b("ys", 0, 512, 2), b("su2", 0, 256), b("su2", 256, 512), A.max)
+        scan("yd mm own", "y2", b("ag"), b("yd"), b("ys"), 0.0, A.mult, A.add)
+        ts("y2", "yt ag0 ag1 ag2 ag3", b("yt", 0, 256), b("ag", 1, 512, 2), 0.5, A.mult)
+        quant("yt", "qy%d" % r, T["qy%d" % r][:, 0:128], T["sqy%d" % r][:, 0:128], b("yt"))
+        order("g", ["qy%d" % r], [], False)
+        if r == 0:
+            g.wait_ge(T.sem["ready"], len(topo.engines(nxt, core)))
+        arr = "arr%d" % r
+        g.remote_dma(T["ld%d" % r][:, 0:64].bitcast(dt.uint8), T["qy%d" % r][:, 0:64].bitcast(dt.uint8), T.sem[arr], T.sem["loc"], pid, rid, mask)
+        g.remote_dma(T["sld%d" % r][:, 0:64], T["sqy%d" % r][:, 0:64], T.sem[arr], T.sem["loc"], pid, rid, mask)
+        nloc[0] += 2 * engines
+        if r == 0:
+            make_arrow_constants()
+        for k in range(2):
+            ts("rf%d" % k, "+av0", b("av", 64 + 32 * k, 92 + 32 * k), rows(k), RND16, A.add, RND16, A.subtract)
+        for k in range(2):
+            for h in range(2):
+                o = 28 * k + 14 * h
+                ts("ie cnt%d" % k, "+eq", b("eq", o, o + 14), b("ie", 0, 14), b("cnt", o + 13, o + 14), A.is_equal)
+        ts("av0", "av1", b("av", 0, 64), b("av", 64, 128), -1.0 / UNIT, A.mult, 0.0, A.max)
+        tt("eq", "ph0", b("ph0"), b("eq", 0, 28), b("eq", 28, 56), A.add)
+        ts("ph0", "av2", b("av", 128, 156), b("ph0"), -2.0, A.mult, 1.0, A.add)
+        for t in (2, 3, 0, 1):
+            act("av%d li" % (0 if t > 1 else 1), "xg%d" % t, b("xg", 224 * t, 224 * t + 224), T.av[:, 32 * t:32 * t + 32].indirect(b("li")))
+            w = (64 + 32 * t) % 128
+            tt("av0 av1 lk xg%d" % t, "+pr", b("st", 2 + t, 1344, 6), T.av[:, w:w + 32].indirect(b("lk")), b("xg", 224 * t, 224 * t + 224), A.mult)
+        act("av2 li", "+sgp", b("sg", 1, 1344, 6), T.av[:, 128:160].indirect(b("li")), -1.0)
+        act("av2 lk", "+sgp", b("sg", 2, 1344, 6), T.av[:, 128:160].indirect(b("lk")))
+        act("yt", "y32", b("y32"), b("yt", 0, 256), 32.0)
+        scan("sgc sgp st1 cst pr", "so", b("so"), b("sg"), b("st"), 0.0, A.mult, A.add)
+        ts("so", "cst", b("st", 0, 1344, 6), b("so", 5, 1344, 6), 3 * UNIT, A.min, -3 * UNIT, A.max)
+        if r == ROUNDS - 1:
+            fill("cwk", b("cw", 512, 513), 0.0)
+            tt("oe0 lane", "oe", b("oe"), b("oe0"), b("lane", 0, 25), A.add)
+            ts("oe", "o1", b("o1"), b("oe"), -6.5, A.add, 1.0 / 14.0, A.mult)
+            ts("o1", "o2", b("o2"), b("o1"), RND0, A.add, RND0, A.subtract)
+            ts("o2", "o3", b("o3"), b("o2"), 2.0, A.mult, 32.5, A.add)
+            tt("o3 oe", "o4", b("o4"), b("o3"), b("oe"), A.add)
+            ts("o4", "loa", b("loa"), b("o4"), 2.0, A.mult)
+        lay_out()
+        if r == ROUNDS - 1:
+            act("ds1 loa", "oa1", b("oa1"), T.ds1[:, 0:1024].indirect(b("loa")), 1.0 / UNIT)
+            dma("y", "oa1", "", T.oa[:, :], b("oa1", 0, 392))
+        order("t", [], ["land%d" % r], False)
+        entry("land%d" % r)[0].append((arr, 2 * len(topo.engines(prv, core)), "remote"))
+        for k in range(4):
+            dst = T.pq[:, 512 * k:512 * k + 128] if k < 2 else T.pp[:, 512 * (k - 2):512 * (k - 2) + 128]
+            tok = ("pq%d" % k) if k < 2 else ("pp%d" % (k - 2))
+            mm("qw sw land%d ld%d" % (r, r), tok, dst, T.qw[:, 128 * k:128 * k + 128], T.sqw[:, 128 * k:128 * k + 128],
+               b("ld%d" % r), b("sld%d" % r))
+        for k in range(4):
+            v = T.pq[:, 512 * k:512 * k + 64] if k < 2 else T.pp[:, 512 * (k - 2):512 * (k - 2) + 64]
+            tok = ("pq%d" % k) if k < 2 else ("pp%d" % (k - 2))
+            tt(tok + " y32", "+wb%d" % (k // 2), b("wb", 64 * k, 64 * k + 64), v, b("y32", k, 256, 4), A.add)
+            if k % 2:
+                o = 64 * k - 64
+                ts("wb%d" % (k // 2), "vv%d" % (k // 2), b("vv", o, o + 128), b("wb", o, o + 128), 0.03125, A.mult)
+                cp("vv%d ox" % (k // 2), ft, T[ft][:, 0:XW].indirect(b("ox", o // 16, o // 16 + 8)), b("vv", o, o + 128))
+        if r == 0:
+            quant("vt", "qv", b("qv"), b("sqv"), b("vt"))
+    qx, sx = quantise_state(3, T[ft], ft, ft)
+    mm("qv qa3", "pd0", T.pd[:, 0:224], b("qv"), b("sqv"), qx[:, 0:224], sx[:, 0:224])
+    mm("qv qb3", "pd1", T.pd[:, 512:736], b("qv"), b("sqv"), qx[:, 224:448], sx[:, 224:448])
+    dma("y", "qa3", "", T.oc[:, 0:896], qx[:, 0:224].bitcast(dt.uint8))
+    act("pd0", "yo0", b("yo", 0, 224), T.pd[:, 0:224])
+    dma("y", "qb3", "", T.oc[:, 896:1792], qx[:, 224:448].bitcast(dt.uint8))
+    cp("pd1", "yo1", b("yo", 224, 448), T.pd[:, 512:736])
+    dma("s", "yo0", "", T.y[:, 0:224], b("yo", 0, 224))
+    dma("s", "yo1", "", T.y[:, 224:448], b("yo", 224, 448))
+    for k in range(4):
+        dma("sy"[k % 2], "qa3 qb3", "", T.osc[4 * k:4 * k + 4, 0:448], sx[32 * k:32 * k + 4, 0:448])
+    g.wait_ge(T.sem["loc"], nloc[0])
+    for k in range(ndma[0]):
+        need("y", "dma%d" % k, 16)
+    for s in ("cv", "cs", "ct", "cg"):
+        need("y", s, count[s])

@@ -1,6 +1,7 @@
 from concourse.mybir import dt, AluOpType, ActivationFunctionType
 
 ROUNDS, C = 3, 448
+CUTS = (0, 160, 320, 448)
 XW = 1936
 UNIT = 65536.0
 MARK = 16384.0
@@ -13,16 +14,17 @@ RND0 = 1.5 * 2.0 ** 23
 F32, B16, I32, U16, QC, U8 = "float32", "bfloat16", "int32", "uint16", "float8_e4m3fn_x4", "uint8"
 SCRATCH = {"pp": ("psum", [128, 1024], F32), "pd": ("psum", [128, 2048], F32), "pq": ("psum", [128, 1024], F32)}
 for _d, _list in [
-        (B16, "xin 1792 ft0 1936 ft1 1936 ft2 1936 ut 512 vt 512 eb 516 ones 516 ie 512 mask 448 rst16 448 rst14 28 sg 1344 "
-              "cw 528 ds0 1024 ds1 1024 ds2 1024 av 160 eq 56 ph0 28 xg 896 st 1344 so 1344 ltb 56 cnt 56 ge 512 rf 1024 "
-              "ag 512 su2 512 ys 512 yd 512 yt 512 y32 256 vv 256"),
-        (F32, "iw 448 r1 448 r2 448 r3 448 ps 448 smk 448 scn 448 oa1 400 wb 256 yo 448 key 113 ep 112 tmn 112 p2 112 capz 112"),
+        (B16, "xin 1792 ft0 1936 ft1 1936 ft2 1936 ut 512 vt 512 eb 516 ones 516 ie 528 mask 448 cap16 448 capf 448 rst14 28 "
+              "sg 1344 cw 528 ds0 1024 ds1 1024 ds2 1024 av 160 eq 56 ph0 28 xg 896 st 1344 so 1344 ltb 56 cnt 56 ge 512 "
+              "rf 1024 ag 512 su2 512 ys 512 yd 512 yt 512 y32 256 vv 256"),
+        (F32, "iw 448 r1 448 r2 448 r3 448 ps 448 smk 448 scn 448 pmf 448 oa1 400 wb 256 yo 448 key 113 ep 112 tmn 112 p2 112 "
+              "capz 112"),
         (I32, "ndin 28 arin 392")]:
     _w = _list.split()
     for _k in range(0, len(_w), 2):
         SCRATCH[_w[_k]] = ("sbuf", [128, int(_w[_k + 1])], _d)
 for _n, _c in [("qw", 512), ("qu", 128), ("qr", 128), ("qv", 128), ("qe", 512), ("qx0", 448), ("qx1", 448), ("qx2", 448),
-               ("qx3", 448), ("qy0", 128), ("qy1", 128), ("qy2", 128), ("ld0", 128), ("ld1", 128), ("ld2", 128)]:
+               ("qx3", 448), ("qy0", 128), ("qy1", 128), ("qy2", 128), ("ld", 256)]:
     SCRATCH[_n] = ("sbuf", [128, _c], QC)
     SCRATCH["s" + _n] = ("sbuf", [128, _c], U8)
 SMALL = {}
@@ -32,7 +34,7 @@ for _buf, _d, _step, _list in [
                            "fm 56 fn 56 fo 56 f1 56 f2 56 f3 56 f4 56 f5 56 f6 56 f7 56 f8 56 f9 56 fa 56 fx 8 lfi 64 oe0 25 oi 16 "
                            "oim 16 ow 4"),
         ("smallu", U16, 16, "lrep 28 lu 8 ndn 28 nd16 28 li 14 lk 14 lc 14 lf 64 loa 25 off 64 ox 16"),
-        ("smallf", F32, 8, "lanef 1 capa 28 capb 30 nd4 28 kb 28 oe 25 o1 25 o2 25 o3 25 o4 25 pm0 28 pm1 30 pen 28 s2 30")]:
+        ("smallf", F32, 8, "lanef 1 capb 30 nd4 28 kb 28 oe 25 o1 25 o2 25 o3 25 o4 25 pm1 30 pen 28 s2 30")]:
     _w, _at = _list.split(), 0
     for _k in range(0, len(_w), 2):
         SMALL[_w[_k]] = (_buf, _at, int(_w[_k + 1]))
@@ -48,7 +50,7 @@ def rank_program(g, core, T, topo):
     if rank is None:
         return
     A = AluOpType
-    COPY = ActivationFunctionType.Copy
+    COPY, SIGN, IDENT = ActivationFunctionType.Copy, ActivationFunctionType.Sign, ActivationFunctionType.Identity
     n = len(T.cores)
     nxt, prv = T.cores[(rank + 1) % n], T.cores[(rank - 1) % n]
 
@@ -126,11 +128,14 @@ def rank_program(g, core, T, topo):
     def scan(R, W, out, d0, d1, init, o0, o1):
         op("v", R, W, lambda e: e.tensor_tensor_scan(out, d0, d1, init, o0, o1))
 
-    def act(R, W, out, in_, scale=1.0):
+    def act(R, W, out, in_, scale=1.0, func=COPY):
         if scale == 1.0:
-            op("s", R, W, lambda e: e.activation(out, in_, COPY))
+            op("s", R, W, lambda e: e.activation(out, in_, func))
         else:
-            op("s", R, W, lambda e: e.activation(out, in_, COPY, scale=scale))
+            op("s", R, W, lambda e: e.activation(out, in_, func, scale=scale))
+
+    def const(W, out, c, cols):
+        op("s", "ie", W, lambda e: e.activation(out, b("ie", 0, cols), IDENT, bias=c, scale=0.0))
 
     def quant(R, W, q, s, in_):
         op("v", R, W, lambda e: e.quantize_mx(q, s, in_))
@@ -154,164 +159,194 @@ def rank_program(g, core, T, topo):
     dma("y", "", "vt", b("vt"), T.v[:, :])
 
     iota("lane0", b("lane0"), [[0, 56]], 0, 1)
-    iota("t28a", b("t28a"), [[224, 2], [1, 14]], 0, 0)
-    iota("iw", b("iw"), [[1, 448]], 0, 0, True)
-    iota("t8", b("t8"), [[16, 8]], 0, 0)
-    iota("ie", b("ie"), [[0, 32], [1, 16]], 0, 0, True)
-    fill("yt", b("yt"), 0.0)
-    for t in range(ROUNDS):
-        quant("yt", "ld%d" % t, b("ld%d" % t), b("sld%d" % t), b("yt"))
-    fill("ones", b("ones"), 1.0)
-    ts("lane0", "lane", b("lane"), b("lane0"), 15, A.bitwise_and)
-    fill("capa", b("capa"), BIG)
-    fill("capb", b("capb"), BIG)
-    ts("lane", "t28b", b("t28b"), b("lane", 0, 28), 14, A.mult)
-    cp("lane", "lanef", b("lanef"), b("lane", 0, 1))
-    fill("rst14", b("rst14"), 1.0)
-    tt("t28b t28a", "t28c", b("t28c"), b("t28b"), b("t28a"), A.add)
-    fill("capz", b("capz"), BIG)
-    fill("key0", b("key", 0, 1), 0.0)
-    cp("t28c", "lrep", b("lrep"), b("t28c"))
-    fill("cwk", b("cw", 512, 528), 0.0)
-    fill("ndw", b("ndw"), 0)
-    fill("s2z", b("s2"), LOW)
-    cp("ndin", "ndn", b("ndn"), b("ndin"))
-    act("iw ndn", "r1", b("r1"), T.iw[:, 0:448].indirect(b("ndn")))
-    cp("t8", "lu", b("lu"), b("t8"))
-    fill("capa", b("capa", 0, 28, 14), -BIG)
-    fill("capb", b("capb", 0, 30, 15), -BIG)
-    fill("rst14", b("rst14", 0, 28, 14), 0.0)
-    fill("capz", b("capz", 0, 112, 14), FLOOR)
-    fill("cwk", b("cw", 512, 513), MARK)
-    for t in range(ROUNDS):
-        fill("fz%d" % t, b("ft%d" % t, 1792, XW), 0.0)
-    ts("ie lanef", "mask", b("mask"), b("ie", 0, 448), b("lanef"), A.is_equal)
-    ts("ie", "rst16", b("rst16"), b("ie", 0, 448), 0.0, A.not_equal)
-
-    iota("h14", b("h14"), [[14, 2], [0, 7]], 0, 0)
-    iota("d14", b("d14"), [[0, 2], [1, 7]], 1, 0)
-    mask = topo.mask(core, prv)
-    rid, pid = topo.addr(prv)[:2]
-    order("g", ["ld0", "ld1", "ld2"], [], False)
-    g.remote_sem_update(T.sem["ready"], T.sem["loc"], pid, rid, mask)
-    nloc = [len(topo.engines(core, prv))]
-    op("g", "ones", "eb", lambda e: e.affine_select(b("eb"), b("ones"), [[-1, 516]], A.is_equal, 0.0, 3, 4))
-    iota("dum0", b("dum0"), [[16, 2]], 449, 0)
-    iota("fj", b("fj"), [[0, 2], [1, 14], [0, 2]], 0, 0)
     iota("fi0", b("fi0"), [[0, 28], [8, 2]], 0, 0)
-    iota("h196", b("h196"), [[196, 2], [0, 7]], 0, 0)
+    iota("fj", b("fj"), [[0, 2], [1, 14], [0, 2]], 0, 0)
+    iota("t28a", b("t28a"), [[224, 2], [1, 14]], 0, 0)
+    iota("d14", b("d14"), [[0, 2], [1, 7]], 1, 0)
     iota("fh", b("fh"), [[112, 2], [0, 28]], 0, 0)
+    iota("t8", b("t8"), [[16, 8]], 0, 0)
+    iota("iw", b("iw"), [[1, 448]], 0, 0, True)
+    iota("ie", b("ie"), [[0, 33], [1, 16]], 0, 0, True)
+    iota("h14", b("h14"), [[14, 2], [0, 7]], 0, 0)
+    iota("h196", b("h196"), [[196, 2], [0, 7]], 0, 0)
     iota("+fx", b("fx", 0, 4), [[32, 2], [8, 2]], 448, 0)
     iota("+fx", b("fx", 4, 8), [[32, 2], [8, 2]], 464, 0)
-    iota("kc", b("kc"), [[0, 2], [-2048, 14]], 14 * 2048, 0)
-    iota("ds0", b("ds0"), [[0, 512], [-1, 2]], 0, 0, True)
-    iota("yc", b("so", 0, 512), [[0, 256], [1, 2]], 0, 0, True) if False else None
-    iota("yd", b("yd"), [[0, 256], [1, 2]], 0, 0, True)
-    iota("oe0", b("oe0"), [[16, 25]], 0, 0)
-    for s, c in ((0, 0), (3, 1), (4, -1), (5, 1)):
-        iota("+sgc", b("sg", s, 1344, 6), [[0, 224]], c, 0, True)
-    iota("st1", b("st", 1, 1344, 6), [[0, 224]], 0, 0, True)
+    iota("dum0", b("dum0"), [[16, 2]], 449, 0)
 
-    quant("ut", "qu", b("qu"), b("squ"), b("ut"))
-    op("v", "qu lu", "qr", lambda e: e.tensor_copy(T.qr[:, 0:128].bitcast(dt.uint32), T.qu[:, 0:128].bitcast(dt.uint32).indirect(b("lu"))))
-    act("qu lu", "sr", b("sqr"), T.squ[:, 0:128].indirect(b("lu")))
-    tt("r1 lrep mask", "r2", b("r2"), T.r1[:, 0:448].indirect(b("lrep")), b("mask"), A.mult)
-    scan("rst16 r2", "r3", b("r3"), b("rst16"), b("r2"), 0.0, A.mult, A.add)
-    for k in range(4):
-        quant("eb", "+qe", T.qe[:, 128 * k:128 * k + 128], T.sqe[:, 128 * k:128 * k + 128], T.eb[:, 3 - k:515 - k])
-    cp("r3", "nd16", b("nd16"), b("r3", 15, 448, 16))
-
-    def quantise_state(r, src, ta, tb):
-        qx, sx = T["qx%d" % r], T["sqx%d" % r]
-        quant(ta, "qa%d" % r, qx[:, 0:224], sx[:, 0:224], src[:, 0:896])
-        quant(tb, "qb%d" % r, qx[:, 224:448], sx[:, 224:448], src[:, 896:1792])
-        return qx, sx
-
-    def begin(r, src, ta, tb):
-        ft = "ft%d" % r
-        qx, sx = quantise_state(r, src, ta, tb)
-        mm("qr sr qa%d" % r, "pp0", T.pp[:, 0:224], b("qr"), b("sqr"), qx[:, 0:224], sx[:, 0:224])
-        mm("qr sr qb%d" % r, "pp1", T.pp[:, 512:736], b("qr"), b("sqr"), qx[:, 224:448], sx[:, 224:448])
-        for k in range(4):
-            mm("qe qa%d qb%d" % (r, r), "pd%d" % k, T.pd[:, 512 * k:512 * k + 448], T.qe[:, 128 * k:128 * k + 128],
-               T.sqe[:, 128 * k:128 * k + 128], qx[:, 0:448], sx[:, 0:448])
-        act("pp0", "ps0", b("ps", 0, 224), T.pp[:, 0:224])
-        for k in range(4):
-            act("pd%d" % k, "+" + ft, b(ft, k, 1792, 4), T.pd[:, 512 * k:512 * k + 448])
-
-    begin(0, T.xin, "xa", "xb")
-    tt("d14 lane", "t14a", b("t14a"), b("d14"), b("lane", 0, 14), A.add)
+    fill("cap16", b("cap16"), BIG)
+    ts("lane0", "lane", b("lane"), b("lane0"), 15, A.bitwise_and)
     ts("lane", "fm", b("fm"), b("lane"), 1, A.arith_shift_right)
     ts("lane", "fn", b("fn"), b("lane"), 1, A.bitwise_and)
-    tt("dum0 lane", "dum", b("dum"), b("dum0"), b("lane", 0, 2), A.add)
-    ts("t14a", "t14b", b("t14b"), b("t14a"), 14, A.is_ge, -14, A.mult)
+    ts("lane", "t28b", b("t28b"), b("lane", 0, 28), 14, A.mult)
     tt("fm fn", "fo", b("fo"), b("fm"), b("fn"), A.subtract)
-    for h in range(2):
-        cp("r3", "+ndw", b("ndw", 16 * h, 16 * h + 14), b("r3", 224 * h + 15, 224 * h + 224, 16))
-    cp("dum", "+ndw", b("ndw", 14, 32, 16), b("dum"))
     ts("lane", "t14e", b("t14e"), b("lane", 0, 14), 14, A.mult)
     ts("fo", "fl", b("fl"), b("fo"), 1, A.add)
-    tt("t14a t14b", "t14c", b("t14c"), b("t14a"), b("t14b"), A.add)
-    ts("ndw", "ndh", b("ndh"), b("ndw"), 4, A.arith_shift_right)
-    ts("ndw", "ndl", b("ndl"), b("ndw"), 15, A.bitwise_and)
+    cp("lane", "lanef", b("lanef"), b("lane", 0, 1))
     tt("fl fi0", "fi", b("fi"), b("fl"), b("fi0"), A.add)
-    tt("t14e h196", "t14f", b("t14f"), b("t14e"), b("h196"), A.add)
-    tt("t14c h14", "t14d", b("t14d"), b("t14c"), b("h14"), A.add)
+    fill("cap16", b("cap16", 0, 448, 16), -BIG)
     tt("fi fj", "f1", b("f1"), b("fi"), b("fj"), A.subtract)
-    tt("t14f t14c", "t14g", b("t14a"), b("t14f"), b("t14c"), A.add)
-    cp("t14d", "lk", b("lk"), b("t14d"))
+    tt("t28b t28a", "t28c", b("t28c"), b("t28b"), b("t28a"), A.add)
     ts("f1", "f2", b("f2"), b("f1"), 0, A.is_lt, 14, A.mult)
-    ts("t14g", "t14h", b("t14b"), b("t14a"), 391, A.min)
-    ts("ndh", "+cwn", b("cw", 448, 480), b("ndh"), 64, A.mult)
+    cp("t28c", "lrep", b("lrep"), b("t28c"))
     tt("f1 f2", "f3", b("f3"), b("f1"), b("f2"), A.add)
-    cp("t14h", "lc", b("lc"), b("t14b"))
-    ts("ndl", "+cwn", b("cw", 480, 512), b("ndl"), 4, A.mult)
+    tt("d14 lane", "t14a", b("t14a"), b("d14"), b("lane", 0, 14), A.add)
     ts("f3", "f4", b("f4"), b("f3"), 16, A.mult, -16, A.add)
     ts("f3", "f6", b("f6"), b("f3"), -16, A.mult, 432, A.add)
+    cp("ndin", "ndn", b("ndn"), b("ndin"))
+    act("iw ndn", "r1", b("r1"), T.iw[:, 0:448].indirect(b("ndn")))
+    const("ones", b("ones"), 1.0, 516)
+    op("g", "ones", "eb", lambda e: e.affine_select(b("eb"), b("ones"), [[-1, 516]], A.is_equal, 0.0, 3, 4))
+    iota("kc", b("kc"), [[0, 2], [-2048, 14]], 14 * 2048, 0)
+    iota("ds0", b("ds0"), [[0, 512], [-1, 2]], 0, 0, True)
     ts("f3", "f8", b("f8"), b("f3"), 7, A.is_le)
     tt("f4 fj", "f5", b("f5"), b("f4"), b("fj"), A.add)
     tt("f6 fi", "f7", b("f7"), b("f6"), b("fi"), A.add)
-    ts("arin lc", "cst", b("st", 0, 1344, 6), T.arin[:, 0:392].indirect(b("lc")), UNIT, A.mult)
+    ts("t14a", "t14b", b("t14b"), b("t14a"), 14, A.is_ge, -14, A.mult)
     tt("f5 f7", "f9", b("f9"), b("f5"), b("f7"), A.subtract)
     ts("f3", "f4", b("f4"), b("f3"), 0, A.is_equal, 512, A.mult)
     tt("f8 f9", "fa", b("fa"), b("f8"), b("f9"), A.mult)
-    ts("fi", "f6", b("f6"), b("fi"), 14, A.is_ge, 513, A.mult)
+    tt("t14a t14b", "t14c", b("t14c"), b("t14a"), b("t14b"), A.add)
     tt("fa f7", "f1", b("f1"), b("fa"), b("f7"), A.add)
-    tt("fx fl", "+lfi", b("lfi", 0, 4), b("fx", 0, 4), b("fl", 0, 4), A.add)
+    ts("fi", "f6", b("f6"), b("fi"), 14, A.is_ge, 513, A.mult)
     tt("f1 fh", "f2", b("f2"), b("f1"), b("fh"), A.add)
-    tt("fx fl", "+lfi", b("lfi", 60, 64), b("fx", 4, 8), b("fl", 0, 4), A.add)
+    cp("t8", "lu", b("lu"), b("t8"))
     tt("f2 f4", "f5", b("f5"), b("f2"), b("f4"), A.max)
-    ts("r3", "nd4", b("nd4"), b("r3", 15, 448, 16), 4.0, A.mult)
+    ts("ie lanef", "mask0", b("mask"), b("ie", 0, 448), b("lanef"), A.is_equal, BIG, A.mult)
     tt("f5 f6", "+lfi", b("lfi", 4, 60), b("f5"), b("f6"), A.max)
-    tt("nd4 kc", "kb", b("kb"), b("nd4"), b("kc"), A.add)
-    cp("lfi", "lf", b("lf"), b("lfi"))
+    quant("ut", "qu", b("qu"), b("squ"), b("ut"))
+    ts("mask0", "mask", b("mask"), b("mask"), LOW, A.add)
+    op("v", "qu lu", "qr", lambda e: e.tensor_copy(T.qr[:, 0:128].bitcast(dt.uint32), T.qu[:, 0:128].bitcast(dt.uint32).indirect(b("lu"))))
+    act("qu lu", "sr", b("sqr"), T.squ[:, 0:128].indirect(b("lu")))
+    tt("r1 lrep mask", "r2", b("r2"), T.r1[:, 0:448].indirect(b("lrep")), b("mask"), A.min)
+    tt("t14e h196", "t14f", b("t14f"), b("t14e"), b("h196"), A.add)
+    scan("cap16 r2", "r3", b("r3"), b("cap16"), b("r2"), 0.0, A.min, A.max)
+    const("yt", b("yt"), 0.0, 512)
+    const("capf", b("capf"), BIG, 448)
+    const("capz", b("capz"), BIG, 112)
+    const("av0 av1 av2", b("av"), 0.0, 160)
+    for h in range(2):
+        act("ie", "+rst14", b("rst14", 14 * h, 14 * h + 14), b("ie", 0, 14), 1.0, SIGN)
+    for t in range(ROUNDS):
+        const("fz%d" % t, b("ft%d" % t, 1792, XW), 0.0, XW - 1792)
 
-    def lay_out():
+    def bank(k, cols):
+        return (T.pp[:, 0:cols], T.pp[:, 512:512 + cols], T.pq[:, 0:cols])[k]
+
+    def quantise_state(r, src, ta, tb):
+        qx, sx = T["qx%d" % r], T["sqx%d" % r]
+        for k in range(3):
+            lo, hi = CUTS[k], CUTS[k + 1]
+            quant((ta, ta + " " + tb, tb)[k], "q%d%d" % (k, r), qx[:, lo:hi], sx[:, lo:hi], src[:, 4 * lo:4 * hi])
+        return qx, sx
+
+    def begin(r, src, ta, tb):
+        qx, sx = quantise_state(r, src, ta, tb)
+        if r == 0:
+            cp("r3", "nd16", b("nd16"), b("r3", 15, 448, 16))
+            for k in range(4):
+                quant("eb", "+qe", T.qe[:, 128 * k:128 * k + 128], T.sqe[:, 128 * k:128 * k + 128], T.eb[:, 3 - k:515 - k])
+        for k in range(3):
+            lo, hi = CUTS[k], CUTS[k + 1]
+            mm("qr sr q%d%d" % (k, r), ("pp0", "pp1", "pq0")[k], bank(k, hi - lo), b("qr"), b("sqr"), qx[:, lo:hi], sx[:, lo:hi])
+        for k in range(4):
+            mm("qe q0%d q1%d q2%d" % (r, r, r), "pd%d" % k, T.pd[:, 512 * k:512 * k + 448], T.qe[:, 128 * k:128 * k + 128],
+               T.sqe[:, 128 * k:128 * k + 128], qx[:, 0:448], sx[:, 0:448])
+        act("pp0", "ps0", b("ps", 0, 160), bank(0, 160))
+        act("pp1", "ps1", b("ps", 160, 320), bank(1, 160))
+
+    def decode(r):
+        ft = "ft%d" % r
+        for k in range(4):
+            act("pd%d" % k, "+" + ft, b(ft, k, 1792, 4), T.pd[:, 512 * k:512 * k + 448])
+
+    def stored():
         act("cst", "cw0", b("cw", 0, 224), b("st", 0, 1344, 6))
         act("cst", "cw1", b("cw", 224, 448), b("st", 0, 1344, 6), -1.0)
+
+    def lay_out():
         act("cw0 cw1 cwk cwn lf", "ds1", b("ds1"), T.cw[:, 0:528].indirect(b("lf")))
 
+    begin(0, T.xin, "xa", "xb")
+    quant("yt", "ldz", b("ld", 128, 256), b("sld", 128, 256), b("yt"))
+    mask = topo.mask(core, prv)
+    rid, pid = topo.addr(prv)[:2]
+    order("g", ["ldz"], [], False)
+    g.remote_sem_update(T.sem["ready"], T.sem["loc"], pid, rid, mask)
+    nloc = [len(topo.engines(core, prv))]
+    iota("yd", b("yd"), [[0, 256], [1, 2]], 0, 0, True)
+    for s, c in ((0, 0), (3, 1), (4, -1), (5, 1)):
+        iota("+sgc", b("sg", s, 1344, 6), [[0, 224]], c, 0, True)
+    iota("st1", b("st", 1, 1344, 6), [[0, 224]], 0, 0, True)
+    iota("oe0", b("oe0"), [[16, 25]], 0, 0)
+    fill("ndw", b("ndw"), 0)
+    tt("t14f t14c", "t14g", b("t14a"), b("t14f"), b("t14c"), A.add)
+    tt("dum0 lane", "dum", b("dum"), b("dum0"), b("lane", 0, 2), A.add)
+    for h in range(2):
+        cp("r3", "+ndw", b("ndw", 16 * h, 16 * h + 14), b("r3", 224 * h + 15, 224 * h + 224, 16))
+    ts("t14g", "t14h", b("t14f"), b("t14a"), 391, A.min)
+    cp("dum", "+ndw", b("ndw", 14, 32, 16), b("dum"))
+    tt("fx fl", "+lfi", b("lfi", 0, 4), b("fx", 0, 4), b("fl", 0, 4), A.add)
+    cp("t14h", "lc", b("lc"), b("t14f"))
+    ts("ndw", "ndh", b("ndh"), b("ndw"), 4, A.arith_shift_right)
+    ts("ndw", "ndl", b("ndl"), b("ndw"), 15, A.bitwise_and)
+    tt("fx fl", "+lfi", b("lfi", 60, 64), b("fx", 4, 8), b("fl", 0, 4), A.add)
+    ts("arin lc", "cst", b("st", 0, 1344, 6), T.arin[:, 0:392].indirect(b("lc")), UNIT, A.mult)
+    stored()
+    fill("cwk", b("cw", 512, 528), 0.0)
+    ts("ndh", "+cwn", b("cw", 448, 480), b("ndh"), 64, A.mult)
+    ts("ndl", "+cwn", b("cw", 480, 512), b("ndl"), 4, A.mult)
+    fill("cwk", b("cw", 512, 513), MARK)
+    cp("lfi", "lf", b("lf"), b("lfi"))
+    fill("capf", b("capf", 0, 448, 224), -BIG)
     lay_out()
-
-    def make_arrow_constants():
-        tt("h14 lane", "t14d", b("t14d"), b("h14"), b("lane", 0, 14), A.add)
-        fill("av0 av1 av2", b("av"), 0.0)
-        cp("t14d", "li", b("li"), b("t14d"))
-
-    def choose(k, pm, wide):
-        o = 28 * k
-        for h in range(2):
-            ts(pm, "+lt%d" % k, b("ltb", o + 14 * h, o + 14 * h + 14), b(pm, wide * h, wide * h + 14), b(pm, wide * h + wide - 1, wide * h + wide), A.is_lt)
-        scan("rst14 lt%d" % k, "cnt%d" % k, b("cnt", o, o + 28), b("rst14"), b("ltb", o, o + 28), 0.0, A.mult, A.add)
-        for h in range(2):
-            ts("ie cnt%d" % k, "+ge", b("ge", 256 * h, 256 * h + 256), b("ie", 256 * h, 256 * h + 256), b("cnt", o + 14 * h + 13, o + 14 * h + 14), A.is_gt)
-        scan("ge ds2", "rf%d" % k, b("rf", 512 * k, 512 * k + 512), b("ge"), b("ds2", 1, 1024, 2), 0.0, A.mult, A.add)
+    decode(0)
 
     def rows(k):
         return b("rf", 512 * k + 46, 512 * k + 46 + 28 * 16 - 15, 16)
 
+    def column(k):
+        ts("rf%d" % k, "+av0", b("av", 64 + 32 * k, 92 + 32 * k), rows(k), RND16, A.add, RND16, A.subtract)
+
+    def turned(k, h):
+        o = 28 * k + 14 * h
+        ts("ie cnt%d" % k, "+eq", b("eq", o, o + 14), b("ie", 0, 14), b("cnt", o + 13, o + 14), A.is_equal)
+
+    def slot(t):
+        ts("ow", "+ox", b("ox", 4 * t, 4 * t + 4), b("ow"), t, A.add)
+
+    def choose(k, tok, pm, beside):
+        o = 28 * k
+        for h in range(2):
+            ts(tok, "+lt%d" % k, b("ltb", o + 14 * h, o + 14 * h + 14), pm(h)[0], pm(h)[1], A.is_lt)
+        beside[0]()
+        scan("rst14 lt%d" % k, "cnt%d" % k, b("cnt", o, o + 28), b("rst14"), b("ltb", o, o + 28), 0.0, A.mult, A.add)
+        beside[1]()
+        for h in range(2):
+            ts("ie cnt%d" % k, "+ge", b("ge", 256 * h, 256 * h + 256), b("ie", 256 * h, 256 * h + 256), b("cnt", o + 14 * h + 13, o + 14 * h + 14), A.is_gt)
+        beside[2]()
+        scan("ge ds2", "rf%d" % k, b("rf", 512 * k, 512 * k + 512), b("ge"), b("ds2", 1, 1024, 2), 0.0, A.mult, A.add)
+
     def differences():
         scan("ds0 ds1", "ds2", b("ds2"), b("ds0"), b("ds1"), 0.0, A.mult, A.add)
+
+    def scores():
+        scan("cap16 smk", "scn", b("scn"), b("cap16"), b("smk"), 0.0, A.min, A.max)
+
+    def nothing():
+        return None
+
+    def late_constants():
+        ts("r3", "nd4", b("nd4"), b("r3", 15, 448, 16), 4.0, A.mult)
+        tt("h14 lane", "t14b", b("t14b"), b("h14"), b("lane", 0, 14), A.add)
+        tt("t14c h14", "t14d", b("t14d"), b("t14c"), b("h14"), A.add)
+        fill("capb", b("capb"), BIG)
+        tt("nd4 kc", "kb", b("kb"), b("nd4"), b("kc"), A.add)
+        fill("s2z", b("s2"), LOW)
+        cp("t14b", "li", b("li"), b("t14b"))
+        cp("t14d", "lk", b("lk"), b("t14d"))
+        fill("capb", b("capb", 0, 30, 15), -BIG)
+        fill("key0", b("key", 0, 1), 0.0)
+        fill("capz", b("capz", 0, 112, 14), FLOOR)
 
     rid, pid = topo.addr(nxt)[:2]
     mask = topo.mask(core, nxt)
@@ -321,72 +356,76 @@ def rank_program(g, core, T, topo):
         ft, fz = "ft%d" % r, "ft%d fz%d" % (r, r)
         if r:
             begin(r, T["ft%d" % (r - 1)], "ft%d" % (r - 1), "ft%d" % (r - 1))
+            decode(r)
             differences()
-        cp("pp1", "ps1", b("ps", 224, 448), T.pp[:, 512:736])
-        tt("ps0 ps1 nd16 mask", "smk", b("smk"), T.ps[:, 0:448].indirect(b("nd16")), b("mask"), A.mult)
-        scan("rst16 smk", "scn", b("scn"), b("rst16"), b("smk"), 0.0, A.mult, A.add)
-        scan("capa scn", "pm0", b("pm0"), b("capa"), b("scn", 15, 448, 16), 0.0, A.min, A.max)
+        cp("pq0", "ps2", b("ps", 320, 448), bank(2, 128))
+        tt("ps0 ps1 ps2 nd16 mask", "smk", b("smk"), T.ps[:, 0:448].indirect(b("nd16")), b("mask"), A.min)
         if r == 0:
-            differences()
-        choose(0, "pm0", 14)
+            late_constants()
+        scan("capf smk", "pmf", b("pmf"), b("capf"), b("smk"), 0.0, A.min, A.max)
+        choose(0, "pmf", lambda h: (b("pmf", 224 * h + 15, 224 * h + 224, 16), b("pmf", 224 * h + 223, 224 * h + 224)),
+               [scores, differences if r == 0 else nothing, nothing])
         ts("rf0", "pen", b("pen"), rows(0), 0.0, A.not_equal, -BIG, A.mult)
-        tt("kb rf0", "+key", b("key", 1, 29), b("kb"), rows(0), A.add)
+        turned(0, 0)
         for h in range(2):
             tt("scn pen s2z", "+s2", b("s2", 15 * h, 15 * h + 14), b("scn", 224 * h + 15, 224 * h + 224, 16), b("pen", 14 * h, 14 * h + 14), A.add)
-        tt("kb rf0", "+key", b("key", 57, 85), b("kb"), rows(0), A.subtract)
+        turned(0, 1)
         scan("capb s2 s2z", "pm1", b("pm1"), b("capb"), b("s2"), 0.0, A.min, A.max)
         tt("rf0", "+ow", b("ow", 0, 2), b("rf", 14, 495, 480), b("rf", 30, 511, 480), A.add)
-        choose(1, "pm1", 15)
-        tt("rf1", "+ow", b("ow", 2, 4), b("rf", 526, 1007, 480), b("rf", 542, 1023, 480), A.add)
+        choose(1, "pm1", lambda h: (b("pm1", 15 * h, 15 * h + 14), b("pm1", 15 * h + 14, 15 * h + 15)),
+               [lambda: tt("kb rf0", "+key", b("key", 1, 29), b("kb"), rows(0), A.add),
+                lambda: tt("kb rf0", "+key", b("key", 57, 85), b("kb"), rows(0), A.subtract), nothing])
+        column(0)
         tt("kb rf1", "+key", b("key", 29, 57), b("kb"), rows(1), A.add)
         tt("kb rf1", "+key", b("key", 85, 113), b("kb"), rows(1), A.subtract)
-        for t in range(4):
-            ts("ow", "+ox", b("ox", 4 * t, 4 * t + 4), b("ow"), t, A.add)
+        tt("rf1", "+ow", b("ow", 2, 4), b("rf", 526, 1007, 480), b("rf", 542, 1023, 480), A.add)
         scan("key key0 capz", "ep", b("ep"), b("key", 0, 112), b("capz"), BIG, A.max, A.min)
-        for t in range(4):
-            act(fz + " ox", "+own", b("ys", 2 * t + 1, 512, 8), T[ft][:, 0:XW].indirect(b("ox", 4 * t, 4 * t + 4)), -2.0)
+        slot(0)
         tt("ep key", "tmn", b("tmn"), b("ep"), b("key", 1, 113), A.min)
         tt("ep key", "+oi", b("oi", 0, 8), b("ep", 13, 112, 14), b("key", 14, 113, 14), A.max)
         scan("capz tmn", "p2", b("p2"), b("capz"), b("tmn"), FLOOR, A.min, A.max)
+        slot(1)
         cp("p2", "+oi", b("oi", 8, 16), b("p2", 13, 112, 14))
+        slot(2)
         ts("oi", "oim", b("oim"), b("oi"), 2047, A.bitwise_and)
+        slot(3)
         for t in range(4):
             ts("oim", "off%d" % t, b("off", 16 * t, 16 * t + 16), b("oim"), t, A.add)
+        column(1)
+        turned(1, 0)
+        ts("av0", "av1", b("av", 0, 64), b("av", 64, 128), -1.0 / UNIT, A.mult, 0.0, A.max)
         for t in range(4):
             act(fz + " off%d" % t, "ag%d" % t, b("ag", t, 512, 4), T[ft][:, 0:XW].indirect(b("off", 16 * t, 16 * t + 8)))
         for t in range(4):
+            act(fz + " ox", "+own", b("ys", 2 * t + 1, 512, 8), T[ft][:, 0:XW].indirect(b("ox", 4 * t, 4 * t + 4)), -2.0)
+        for t in (2, 3, 0, 1):
+            act("av%d li" % (0 if t > 1 else 1), "xg%d" % t, b("xg", 224 * t, 224 * t + 224), T.av[:, 32 * t:32 * t + 32].indirect(b("li")))
+        for t in range(4):
             tt(fz + " off%d ag%d" % (t, t), "+su", b("su2", t, 512, 4), T[ft][:, 0:XW].indirect(b("off", 16 * t + 8, 16 * t + 16)), b("ag", t, 512, 4), A.add)
+        turned(1, 1)
         tt("su", "mm", b("ys", 0, 512, 2), b("su2", 0, 256), b("su2", 256, 512), A.max)
+        tt("eq", "ph0", b("ph0"), b("eq", 0, 28), b("eq", 28, 56), A.add)
         scan("yd mm own", "y2", b("ag"), b("yd"), b("ys"), 0.0, A.mult, A.add)
+        ts("ph0", "av2", b("av", 128, 156), b("ph0"), -2.0, A.mult, 1.0, A.add)
+        act("av2 li", "+sgp", b("sg", 1, 1344, 6), T.av[:, 128:160].indirect(b("li")), -1.0)
+        act("av2 lk", "+sgp", b("sg", 2, 1344, 6), T.av[:, 128:160].indirect(b("lk")))
         ts("y2", "yt ag0 ag1 ag2 ag3", b("yt", 0, 256), b("ag", 1, 512, 2), 0.5, A.mult)
         quant("yt", "qy%d" % r, T["qy%d" % r][:, 0:128], T["sqy%d" % r][:, 0:128], b("yt"))
         order("g", ["qy%d" % r], [], False)
         if r == 0:
             g.wait_ge(T.sem["ready"], len(topo.engines(nxt, core)))
-        arr = "arr%d" % r
-        g.remote_dma(T["ld%d" % r][:, 0:64].bitcast(dt.uint8), T["qy%d" % r][:, 0:64].bitcast(dt.uint8), T.sem[arr], T.sem["loc"], pid, rid, mask)
-        g.remote_dma(T["sld%d" % r][:, 0:64], T["sqy%d" % r][:, 0:64], T.sem[arr], T.sem["loc"], pid, rid, mask)
+        arr, at = "arr%d" % r, 64 * (ROUNDS - 1 - r)
+        g.remote_dma(T.ld[:, at:at + 64].bitcast(dt.uint8), T["qy%d" % r][:, 0:64].bitcast(dt.uint8), T.sem[arr], T.sem["loc"], pid, rid, mask)
+        g.remote_dma(T.sld[:, at:at + 64], T["sqy%d" % r][:, 0:64], T.sem[arr], T.sem["loc"], pid, rid, mask)
         nloc[0] += 2 * engines
-        if r == 0:
-            make_arrow_constants()
-        for k in range(2):
-            ts("rf%d" % k, "+av0", b("av", 64 + 32 * k, 92 + 32 * k), rows(k), RND16, A.add, RND16, A.subtract)
-        for k in range(2):
-            for h in range(2):
-                o = 28 * k + 14 * h
-                ts("ie cnt%d" % k, "+eq", b("eq", o, o + 14), b("ie", 0, 14), b("cnt", o + 13, o + 14), A.is_equal)
-        ts("av0", "av1", b("av", 0, 64), b("av", 64, 128), -1.0 / UNIT, A.mult, 0.0, A.max)
-        tt("eq", "ph0", b("ph0"), b("eq", 0, 28), b("eq", 28, 56), A.add)
-        ts("ph0", "av2", b("av", 128, 156), b("ph0"), -2.0, A.mult, 1.0, A.add)
         for t in (2, 3, 0, 1):
-            act("av%d li" % (0 if t > 1 else 1), "xg%d" % t, b("xg", 224 * t, 224 * t + 224), T.av[:, 32 * t:32 * t + 32].indirect(b("li")))
             w = (64 + 32 * t) % 128
             tt("av0 av1 lk xg%d" % t, "+pr", b("st", 2 + t, 1344, 6), T.av[:, w:w + 32].indirect(b("lk")), b("xg", 224 * t, 224 * t + 224), A.mult)
-        act("av2 li", "+sgp", b("sg", 1, 1344, 6), T.av[:, 128:160].indirect(b("li")), -1.0)
-        act("av2 lk", "+sgp", b("sg", 2, 1344, 6), T.av[:, 128:160].indirect(b("lk")))
         act("yt", "y32", b("y32"), b("yt", 0, 256), 32.0)
         scan("sgc sgp st1 cst pr", "so", b("so"), b("sg"), b("st"), 0.0, A.mult, A.add)
         ts("so", "cst", b("st", 0, 1344, 6), b("so", 5, 1344, 6), 3 * UNIT, A.min, -3 * UNIT, A.max)
+        if r == 0:
+            quant("vt", "qv", b("qv"), b("sqv"), b("vt"))
         if r == ROUNDS - 1:
             fill("cwk", b("cw", 512, 513), 0.0)
             tt("oe0 lane", "oe", b("oe"), b("oe0"), b("lane", 0, 25), A.add)
@@ -395,38 +434,51 @@ def rank_program(g, core, T, topo):
             ts("o2", "o3", b("o3"), b("o2"), 2.0, A.mult, 32.5, A.add)
             tt("o3 oe", "o4", b("o4"), b("o3"), b("oe"), A.add)
             ts("o4", "loa", b("loa"), b("o4"), 2.0, A.mult)
+        stored()
         lay_out()
         if r == ROUNDS - 1:
             act("ds1 loa", "oa1", b("oa1"), T.ds1[:, 0:1024].indirect(b("loa")), 1.0 / UNIT)
             dma("y", "oa1", "", T.oa[:, :], b("oa1", 0, 392))
         order("t", [], ["land%d" % r], False)
         entry("land%d" % r)[0].append((arr, 2 * len(topo.engines(prv, core)), "remote"))
+        toks = ("pq0", "pq1", "pp0", "pp1")
+
+        def place(k, cols):
+            return T.pq[:, 512 * k:512 * k + cols] if k < 2 else T.pp[:, 512 * (k - 2):512 * (k - 2) + cols]
+
+        def sum_(k):
+            tt(toks[k] + " y32", "+wb%d" % (k // 2), b("wb", 64 * k, 64 * k + 64), place(k, 64), b("y32", k, 256, 4), A.add)
+
+        def scaled(k):
+            ts("wb%d" % k, "vv%d" % k, b("vv", 128 * k, 128 * k + 128), b("wb", 128 * k, 128 * k + 128), 0.03125, A.mult)
+
+        def scatter(k):
+            cp("vv%d ox" % k, ft, T[ft][:, 0:XW].indirect(b("ox", 8 * k, 8 * k + 8)), b("vv", 128 * k, 128 * k + 128))
+
         for k in range(4):
-            dst = T.pq[:, 512 * k:512 * k + 128] if k < 2 else T.pp[:, 512 * (k - 2):512 * (k - 2) + 128]
-            tok = ("pq%d" % k) if k < 2 else ("pp%d" % (k - 2))
-            mm("qw sw land%d ld%d" % (r, r), tok, dst, T.qw[:, 128 * k:128 * k + 128], T.sqw[:, 128 * k:128 * k + 128],
-               b("ld%d" % r), b("sld%d" % r))
-        for k in range(4):
-            v = T.pq[:, 512 * k:512 * k + 64] if k < 2 else T.pp[:, 512 * (k - 2):512 * (k - 2) + 64]
-            tok = ("pq%d" % k) if k < 2 else ("pp%d" % (k - 2))
-            tt(tok + " y32", "+wb%d" % (k // 2), b("wb", 64 * k, 64 * k + 64), v, b("y32", k, 256, 4), A.add)
-            if k % 2:
-                o = 64 * k - 64
-                ts("wb%d" % (k // 2), "vv%d" % (k // 2), b("vv", o, o + 128), b("wb", o, o + 128), 0.03125, A.mult)
-                cp("vv%d ox" % (k // 2), ft, T[ft][:, 0:XW].indirect(b("ox", o // 16, o // 16 + 8)), b("vv", o, o + 128))
-        if r == 0:
-            quant("vt", "qv", b("qv"), b("sqv"), b("vt"))
+            mm("qw sw ldz land%d" % r, toks[k], place(k, 128), T.qw[:, 128 * k:128 * k + 128], T.sqw[:, 128 * k:128 * k + 128],
+               b("ld", at, at + 128), b("sld", at, at + 128))
+        sum_(0)
+        sum_(1)
+        sum_(2)
+        scaled(0)
+        sum_(3)
+        scatter(0)
+        scaled(1)
+        scatter(1)
     qx, sx = quantise_state(3, T[ft], ft, ft)
-    mm("qv qa3", "pd0", T.pd[:, 0:224], b("qv"), b("sqv"), qx[:, 0:224], sx[:, 0:224])
-    mm("qv qb3", "pd1", T.pd[:, 512:736], b("qv"), b("sqv"), qx[:, 224:448], sx[:, 224:448])
-    dma("y", "qa3", "", T.oc[:, 0:896], qx[:, 0:224].bitcast(dt.uint8))
-    act("pd0", "yo0", b("yo", 0, 224), T.pd[:, 0:224])
-    dma("y", "qb3", "", T.oc[:, 896:1792], qx[:, 224:448].bitcast(dt.uint8))
-    cp("pd1", "yo1", b("yo", 224, 448), T.pd[:, 512:736])
-    dma("s", "yo0", "", T.y[:, 0:224], b("yo", 0, 224))
-    dma("s", "yo1", "", T.y[:, 224:448], b("yo", 224, 448))
+    for k in range(3):
+        lo, hi = CUTS[k], CUTS[k + 1]
+        mm("qv q%d3" % k, ("pp0", "pp1", "pq0")[k], bank(k, hi - lo), b("qv"), b("sqv"), qx[:, lo:hi], sx[:, lo:hi])
+    act("pp0", "yo0", b("yo", 0, 160), bank(0, 160))
+    act("pp1", "yo1", b("yo", 160, 320), bank(1, 160))
+    cp("pq0", "yo2", b("yo", 320, 448), bank(2, 128))
+    dma("y", "q03 q13", "", T.oc[:, 0:1280], qx[:, 0:320].bitcast(dt.uint8))
+    dma("s", "yo0 yo1", "", T.y[:, 0:320], b("yo", 0, 320))
+    dma("y", "yo2", "", T.y[:, 320:448], b("yo", 320, 448))
+    dma("s", "q23", "", T.oc[:, 1280:1792], qx[:, 320:448].bitcast(dt.uint8))
     for k in range(4):
-        dma("sy"[k % 2], "qa3 qb3", "", T.osc[4 * k:4 * k + 4, 0:448], sx[32 * k:32 * k + 4, 0:448])
+        dma("sy"[k % 2], "q03 q13 q23", "", T.osc[4 * k:4 * k + 4, 0:448], sx[32 * k:32 * k + 4, 0:448])
     g.wait_ge(T.sem["loc"], nloc[0])
     for k in range(ndma[0]):
         need("y", "dma%d" % k, 16)

from concourse.mybir import dt, AluOpType, ActivationFunctionType

ROUNDS, C = 3, 448
CUTS = (0, 160, 320, 448)
XW = 1936
UNIT = 65536.0
MARK = 16384.0
FLOOR = 65536.0 + 4 * 448
BIG = 2.0 ** 99
LOW = -(2.0 ** 98)
RND16 = 1.5 * 2.0 ** 39
RND0 = 1.5 * 2.0 ** 23

F32, B16, I32, U16, QC, U8 = "float32", "bfloat16", "int32", "uint16", "float8_e4m3fn_x4", "uint8"
SCRATCH = {"pp": ("psum", [128, 1024], F32), "pd": ("psum", [128, 2048], F32), "pq": ("psum", [128, 1024], F32)}
for _d, _list in [
        (B16, "xin 1792 ft0 1936 ft1 1936 ft2 1936 ut 512 vt 512 eb 516 ones 516 ie 528 mask 448 cap16 448 capf 448 rst14 28 "
              "sg 1344 cw 528 ds0 1024 ds1 1024 ds2 1024 av 160 eq 56 ph0 28 xg 896 st 1344 so 1344 ltb 56 cnt 56 ge 512 "
              "rf 1024 ag 512 su2 512 ys 512 yd 512 yt 512 y32 256 vv 256"),
        (F32, "iw 448 r1 448 r2 448 r3 448 ps 448 smk 448 scn 448 pmf 448 oa1 400 wb 256 yo 448 key 113 ep 112 tmn 112 p2 112 "
              "capz 112"),
        (I32, "ndin 28 arin 392")]:
    _w = _list.split()
    for _k in range(0, len(_w), 2):
        SCRATCH[_w[_k]] = ("sbuf", [128, int(_w[_k + 1])], _d)
for _n, _c in [("qw", 512), ("qu", 128), ("qr", 128), ("qv", 128), ("qe", 512), ("qx0", 448), ("qx1", 448), ("qx2", 448),
               ("qx3", 448), ("qy0", 128), ("qy1", 128), ("qy2", 128), ("ld", 256)]:
    SCRATCH[_n] = ("sbuf", [128, _c], QC)
    SCRATCH["s" + _n] = ("sbuf", [128, _c], U8)
SMALL = {}
for _buf, _d, _step, _list in [
        ("smalli", I32, 8, "lane0 56 lane 56 t28a 28 t28b 28 t28c 28 t8 8 ndw 32 ndh 32 ndl 32 dum 2 dum0 2 kc 28 h14 14 d14 14 "
                           "h196 14 t14a 14 t14b 14 t14c 14 t14d 14 t14e 14 t14f 14 fj 56 fh 56 fi0 56 fi 56 fl 56 "
                           "fm 56 fn 56 fo 56 f1 56 f2 56 f3 56 f4 56 f5 56 f6 56 f7 56 f8 56 f9 56 fa 56 fx 8 lfi 64 oe0 25 oi 16 "
                           "oim 16 ow 4"),
        ("smallu", U16, 16, "lrep 28 lu 8 ndn 28 nd16 28 li 14 lk 14 lc 14 lf 64 loa 25 off 64 ox 16"),
        ("smallf", F32, 8, "lanef 1 capb 30 nd4 28 kb 28 oe 25 o1 25 o2 25 o3 25 o4 25 pm1 30 pen 28 s2 30")]:
    _w, _at = _list.split(), 0
    for _k in range(0, len(_w), 2):
        SMALL[_w[_k]] = (_buf, _at, int(_w[_k + 1]))
        _at += (int(_w[_k + 1]) + _step - 1) // _step * _step
    SCRATCH[_buf] = ("sbuf", [128, _at], _d)

NDMA = 24
SEMAPHORES = ["cv", "cs", "ct", "cg", "ready", "loc", "arr0", "arr1", "arr2"] + ["dma%d" % _k for _k in range(NDMA)]


def rank_program(g, core, T, topo):
    rank = T.rank_of(core)
    if rank is None:
        return
    A = AluOpType
    COPY, SIGN, IDENT = ActivationFunctionType.Copy, ActivationFunctionType.Sign, ActivationFunctionType.Identity
    n = len(T.cores)
    nxt, prv = T.cores[(rank + 1) % n], T.cores[(rank - 1) % n]

    queue = {"v": g.vector, "s": g.scalar, "t": g.tensor, "g": g, "y": g.sync}
    semof = {"v": "cv", "s": "cs", "t": "ct", "g": "cg"}
    count = {"cv": 0, "cs": 0, "ct": 0, "cg": 0}
    state, seen, ndma = {}, {}, [0]

    def entry(t):
        return state.setdefault(t, [[], [], [], True])

    def need(q, sem, val):
        if seen.get((q, sem), 0) < val:
            queue[q].wait_ge(T.sem[sem], val)
            seen[(q, sem)] = val

    def order(q, R, W, dma):
        want = []
        for t in R:
            want += entry(t)[0]
        for t in W:
            s = entry(t.lstrip("+"))
            if t[0] != "+" or s[1] or s[3]:
                s[2] = s[0] + [e for e in s[1] if dma or e[2] != q]
                s[0], s[1], s[3] = [], [], t[0] != "+"
            want += s[2]
        most = {}
        for sem, val, w in want:
            most[sem] = max(most.get(sem, 0), val)
        for sem in most:
            need(q, sem, most[sem])

    def note(R, W, e):
        for t in R:
            entry(t)[1].append(e)
        for t in W:
            entry(t.lstrip("+"))[0].append(e)

    def op(q, R, W, f):
        R, W = R.split(), W.split()
        order(q, R, W, False)
        s = semof[q]
        count[s] += 1
        f(queue[q]).then_inc(T.sem[s], 1)
        note(R, W, (s, count[s], q))

    def dma(q, R, W, out, in_):
        R, W = R.split(), W.split()
        order(q, R, W, True)
        s = "dma%d" % ndma[0]
        ndma[0] += 1
        queue[q].dma_start(out, in_).then_inc(T.sem[s], 16)
        note(R, W, (s, 16, "dma"))

    def b(name, lo=0, hi=None, step=1):
        buf, at, cols = SMALL[name] if name in SMALL else (name, 0, SCRATCH[name][1][1])
        hi = cols if hi is None else hi
        return T[buf][:, at + lo:at + hi:step] if step > 1 else T[buf][:, at + lo:at + hi]

    def ts(R, W, out, in0, s1, op0, s2=None, op1=None):
        if op1 is None:
            op("v", R, W, lambda e: e.tensor_scalar(out, in0, s1, None, op0))
        else:
            op("v", R, W, lambda e: e.tensor_scalar(out, in0, s1, s2, op0, op1))

    def tt(R, W, out, in0, in1, o):
        op("v", R, W, lambda e: e.tensor_tensor(out, in0, in1, o))

    def cp(R, W, out, in_):
        op("v", R, W, lambda e: e.tensor_copy(out, in_))

    def fill(W, out, c):
        op("v", "", W, lambda e: e.memset(out, c))

    def scan(R, W, out, d0, d1, init, o0, o1):
        op("v", R, W, lambda e: e.tensor_tensor_scan(out, d0, d1, init, o0, o1))

    def act(R, W, out, in_, scale=1.0, func=COPY):
        if scale == 1.0:
            op("s", R, W, lambda e: e.activation(out, in_, func))
        else:
            op("s", R, W, lambda e: e.activation(out, in_, func, scale=scale))

    def const(W, out, c, cols):
        op("s", "ie", W, lambda e: e.activation(out, b("ie", 0, cols), IDENT, bias=c, scale=0.0))

    def quant(R, W, q, s, in_):
        op("v", R, W, lambda e: e.quantize_mx(q, s, in_))

    def mm(R, W, out, a, sa, m, sm):
        op("t", R, W, lambda e: e.matmul_mx(out, a, sa, m, sm, True, True))

    def iota(W, out, pattern, base, cm, small=False):
        if small:
            op("g", "", W, lambda e: e.iota(out, pattern, base, cm, allow_small_or_imprecise_dtypes=True))
        else:
            op("g", "", W, lambda e: e.iota(out, pattern, base, cm))

    dma("y", "", "ndin", b("ndin"), T.nd[:, :])
    dma("s", "", "xb", b("xin", 896, 1792), T.x[:, 896:1792])
    dma("y", "", "ut", b("ut"), T.u[:, :])
    dma("y", "", "xa", b("xin", 0, 896), T.x[:, 0:896])
    dma("y", "", "arin", b("arin"), T.ar[:, :])
    dma("y", "", "sw", b("sqw"), T.ws[:, :])
    dma("y", "", "qw", T.qw[:, :].bitcast(dt.uint8), T.wc[:, :])
    dma("y", "", "vt", b("vt"), T.v[:, :])

    iota("lane0", b("lane0"), [[0, 56]], 0, 1)
    iota("fi0", b("fi0"), [[0, 28], [8, 2]], 0, 0)
    iota("fj", b("fj"), [[0, 2], [1, 14], [0, 2]], 0, 0)
    iota("t28a", b("t28a"), [[224, 2], [1, 14]], 0, 0)
    iota("d14", b("d14"), [[0, 2], [1, 7]], 1, 0)
    iota("fh", b("fh"), [[112, 2], [0, 28]], 0, 0)
    iota("t8", b("t8"), [[16, 8]], 0, 0)
    iota("iw", b("iw"), [[1, 448]], 0, 0, True)
    iota("ie", b("ie"), [[0, 33], [1, 16]], 0, 0, True)
    iota("h14", b("h14"), [[14, 2], [0, 7]], 0, 0)
    iota("h196", b("h196"), [[196, 2], [0, 7]], 0, 0)
    iota("+fx", b("fx", 0, 4), [[32, 2], [8, 2]], 448, 0)
    iota("+fx", b("fx", 4, 8), [[32, 2], [8, 2]], 464, 0)
    iota("dum0", b("dum0"), [[16, 2]], 449, 0)

    fill("cap16", b("cap16"), BIG)
    ts("lane0", "lane", b("lane"), b("lane0"), 15, A.bitwise_and)
    ts("lane", "fm", b("fm"), b("lane"), 1, A.arith_shift_right)
    ts("lane", "fn", b("fn"), b("lane"), 1, A.bitwise_and)
    ts("lane", "t28b", b("t28b"), b("lane", 0, 28), 14, A.mult)
    tt("fm fn", "fo", b("fo"), b("fm"), b("fn"), A.subtract)
    ts("lane", "t14e", b("t14e"), b("lane", 0, 14), 14, A.mult)
    ts("fo", "fl", b("fl"), b("fo"), 1, A.add)
    cp("lane", "lanef", b("lanef"), b("lane", 0, 1))
    tt("fl fi0", "fi", b("fi"), b("fl"), b("fi0"), A.add)
    fill("cap16", b("cap16", 0, 448, 16), -BIG)
    tt("fi fj", "f1", b("f1"), b("fi"), b("fj"), A.subtract)
    tt("t28b t28a", "t28c", b("t28c"), b("t28b"), b("t28a"), A.add)
    ts("f1", "f2", b("f2"), b("f1"), 0, A.is_lt, 14, A.mult)
    cp("t28c", "lrep", b("lrep"), b("t28c"))
    tt("f1 f2", "f3", b("f3"), b("f1"), b("f2"), A.add)
    tt("d14 lane", "t14a", b("t14a"), b("d14"), b("lane", 0, 14), A.add)
    ts("f3", "f4", b("f4"), b("f3"), 16, A.mult, -16, A.add)
    ts("f3", "f6", b("f6"), b("f3"), -16, A.mult, 432, A.add)
    cp("ndin", "ndn", b("ndn"), b("ndin"))
    act("iw ndn", "r1", b("r1"), T.iw[:, 0:448].indirect(b("ndn")))
    const("ones", b("ones"), 1.0, 516)
    op("g", "ones", "eb", lambda e: e.affine_select(b("eb"), b("ones"), [[-1, 516]], A.is_equal, 0.0, 3, 4))
    iota("kc", b("kc"), [[0, 2], [-2048, 14]], 14 * 2048, 0)
    iota("ds0", b("ds0"), [[0, 512], [-1, 2]], 0, 0, True)
    ts("f3", "f8", b("f8"), b("f3"), 7, A.is_le)
    tt("f4 fj", "f5", b("f5"), b("f4"), b("fj"), A.add)
    tt("f6 fi", "f7", b("f7"), b("f6"), b("fi"), A.add)
    ts("t14a", "t14b", b("t14b"), b("t14a"), 14, A.is_ge, -14, A.mult)
    tt("f5 f7", "f9", b("f9"), b("f5"), b("f7"), A.subtract)
    ts("f3", "f4", b("f4"), b("f3"), 0, A.is_equal, 512, A.mult)
    tt("f8 f9", "fa", b("fa"), b("f8"), b("f9"), A.mult)
    tt("t14a t14b", "t14c", b("t14c"), b("t14a"), b("t14b"), A.add)
    tt("fa f7", "f1", b("f1"), b("fa"), b("f7"), A.add)
    ts("fi", "f6", b("f6"), b("fi"), 14, A.is_ge, 513, A.mult)
    tt("f1 fh", "f2", b("f2"), b("f1"), b("fh"), A.add)
    cp("t8", "lu", b("lu"), b("t8"))
    tt("f2 f4", "f5", b("f5"), b("f2"), b("f4"), A.max)
    ts("ie lanef", "mask0", b("mask"), b("ie", 0, 448), b("lanef"), A.is_equal, BIG, A.mult)
    tt("f5 f6", "+lfi", b("lfi", 4, 60), b("f5"), b("f6"), A.max)
    quant("ut", "qu", b("qu"), b("squ"), b("ut"))
    ts("mask0", "mask", b("mask"), b("mask"), LOW, A.add)
    op("v", "qu lu", "qr", lambda e: e.tensor_copy(T.qr[:, 0:128].bitcast(dt.uint32), T.qu[:, 0:128].bitcast(dt.uint32).indirect(b("lu"))))
    act("qu lu", "sr", b("sqr"), T.squ[:, 0:128].indirect(b("lu")))
    tt("r1 lrep mask", "r2", b("r2"), T.r1[:, 0:448].indirect(b("lrep")), b("mask"), A.min)
    tt("t14e h196", "t14f", b("t14f"), b("t14e"), b("h196"), A.add)
    scan("cap16 r2", "r3", b("r3"), b("cap16"), b("r2"), 0.0, A.min, A.max)
    const("yt", b("yt"), 0.0, 512)
    const("capf", b("capf"), BIG, 448)
    const("capz", b("capz"), BIG, 112)
    const("av0 av1 av2", b("av"), 0.0, 160)
    for h in range(2):
        act("ie", "+rst14", b("rst14", 14 * h, 14 * h + 14), b("ie", 0, 14), 1.0, SIGN)
    for t in range(ROUNDS):
        const("fz%d" % t, b("ft%d" % t, 1792, XW), 0.0, XW - 1792)

    def bank(k, cols):
        return (T.pp[:, 0:cols], T.pp[:, 512:512 + cols], T.pq[:, 0:cols])[k]

    def quantise_state(r, src, ta, tb):
        qx, sx = T["qx%d" % r], T["sqx%d" % r]
        for k in range(3):
            lo, hi = CUTS[k], CUTS[k + 1]
            quant((ta, ta + " " + tb, tb)[k], "q%d%d" % (k, r), qx[:, lo:hi], sx[:, lo:hi], src[:, 4 * lo:4 * hi])
        return qx, sx

    def begin(r, src, ta, tb):
        qx, sx = quantise_state(r, src, ta, tb)
        if r == 0:
            cp("r3", "nd16", b("nd16"), b("r3", 15, 448, 16))
            for k in range(4):
                quant("eb", "+qe", T.qe[:, 128 * k:128 * k + 128], T.sqe[:, 128 * k:128 * k + 128], T.eb[:, 3 - k:515 - k])
        for k in range(3):
            lo, hi = CUTS[k], CUTS[k + 1]
            mm("qr sr q%d%d" % (k, r), ("pp0", "pp1", "pq0")[k], bank(k, hi - lo), b("qr"), b("sqr"), qx[:, lo:hi], sx[:, lo:hi])
        for k in range(4):
            mm("qe q0%d q1%d q2%d" % (r, r, r), "pd%d" % k, T.pd[:, 512 * k:512 * k + 448], T.qe[:, 128 * k:128 * k + 128],
               T.sqe[:, 128 * k:128 * k + 128], qx[:, 0:448], sx[:, 0:448])
        act("pp0", "ps0", b("ps", 0, 160), bank(0, 160))
        act("pp1", "ps1", b("ps", 160, 320), bank(1, 160))

    def decode(r):
        ft = "ft%d" % r
        for k in range(4):
            act("pd%d" % k, "+" + ft, b(ft, k, 1792, 4), T.pd[:, 512 * k:512 * k + 448])

    def stored():
        act("cst", "cw0", b("cw", 0, 224), b("st", 0, 1344, 6))
        act("cst", "cw1", b("cw", 224, 448), b("st", 0, 1344, 6), -1.0)

    def lay_out():
        act("cw0 cw1 cwk cwn lf", "ds1", b("ds1"), T.cw[:, 0:528].indirect(b("lf")))

    begin(0, T.xin, "xa", "xb")
    quant("yt", "ldz", b("ld", 128, 256), b("sld", 128, 256), b("yt"))
    mask = topo.mask(core, prv)
    rid, pid = topo.addr(prv)[:2]
    order("g", ["ldz"], [], False)
    g.remote_sem_update(T.sem["ready"], T.sem["loc"], pid, rid, mask)
    nloc = [len(topo.engines(core, prv))]
    iota("yd", b("yd"), [[0, 256], [1, 2]], 0, 0, True)
    for s, c in ((0, 0), (3, 1), (4, -1), (5, 1)):
        iota("+sgc", b("sg", s, 1344, 6), [[0, 224]], c, 0, True)
    iota("st1", b("st", 1, 1344, 6), [[0, 224]], 0, 0, True)
    iota("oe0", b("oe0"), [[16, 25]], 0, 0)
    fill("ndw", b("ndw"), 0)
    tt("t14f t14c", "t14g", b("t14a"), b("t14f"), b("t14c"), A.add)
    tt("dum0 lane", "dum", b("dum"), b("dum0"), b("lane", 0, 2), A.add)
    for h in range(2):
        cp("r3", "+ndw", b("ndw", 16 * h, 16 * h + 14), b("r3", 224 * h + 15, 224 * h + 224, 16))
    ts("t14g", "t14h", b("t14f"), b("t14a"), 391, A.min)
    cp("dum", "+ndw", b("ndw", 14, 32, 16), b("dum"))
    tt("fx fl", "+lfi", b("lfi", 0, 4), b("fx", 0, 4), b("fl", 0, 4), A.add)
    cp("t14h", "lc", b("lc"), b("t14f"))
    ts("ndw", "ndh", b("ndh"), b("ndw"), 4, A.arith_shift_right)
    ts("ndw", "ndl", b("ndl"), b("ndw"), 15, A.bitwise_and)
    tt("fx fl", "+lfi", b("lfi", 60, 64), b("fx", 4, 8), b("fl", 0, 4), A.add)
    ts("arin lc", "cst", b("st", 0, 1344, 6), T.arin[:, 0:392].indirect(b("lc")), UNIT, A.mult)
    stored()
    fill("cwk", b("cw", 512, 528), 0.0)
    ts("ndh", "+cwn", b("cw", 448, 480), b("ndh"), 64, A.mult)
    ts("ndl", "+cwn", b("cw", 480, 512), b("ndl"), 4, A.mult)
    fill("cwk", b("cw", 512, 513), MARK)
    cp("lfi", "lf", b("lf"), b("lfi"))
    fill("capf", b("capf", 0, 448, 224), -BIG)
    lay_out()
    decode(0)

    def rows(k):
        return b("rf", 512 * k + 46, 512 * k + 46 + 28 * 16 - 15, 16)

    def column(k):
        ts("rf%d" % k, "+av0", b("av", 64 + 32 * k, 92 + 32 * k), rows(k), RND16, A.add, RND16, A.subtract)

    def turned(k, h):
        o = 28 * k + 14 * h
        ts("ie cnt%d" % k, "+eq", b("eq", o, o + 14), b("ie", 0, 14), b("cnt", o + 13, o + 14), A.is_equal)

    def slot(t):
        ts("ow", "+ox", b("ox", 4 * t, 4 * t + 4), b("ow"), t, A.add)

    def choose(k, tok, pm, beside):
        o = 28 * k
        for h in range(2):
            ts(tok, "+lt%d" % k, b("ltb", o + 14 * h, o + 14 * h + 14), pm(h)[0], pm(h)[1], A.is_lt)
        beside[0]()
        scan("rst14 lt%d" % k, "cnt%d" % k, b("cnt", o, o + 28), b("rst14"), b("ltb", o, o + 28), 0.0, A.mult, A.add)
        beside[1]()
        for h in range(2):
            ts("ie cnt%d" % k, "+ge", b("ge", 256 * h, 256 * h + 256), b("ie", 256 * h, 256 * h + 256), b("cnt", o + 14 * h + 13, o + 14 * h + 14), A.is_gt)
        beside[2]()
        scan("ge ds2", "rf%d" % k, b("rf", 512 * k, 512 * k + 512), b("ge"), b("ds2", 1, 1024, 2), 0.0, A.mult, A.add)

    def differences():
        scan("ds0 ds1", "ds2", b("ds2"), b("ds0"), b("ds1"), 0.0, A.mult, A.add)

    def scores():
        scan("cap16 smk", "scn", b("scn"), b("cap16"), b("smk"), 0.0, A.min, A.max)

    def nothing():
        return None

    def late_constants():
        ts("r3", "nd4", b("nd4"), b("r3", 15, 448, 16), 4.0, A.mult)
        tt("h14 lane", "t14b", b("t14b"), b("h14"), b("lane", 0, 14), A.add)
        tt("t14c h14", "t14d", b("t14d"), b("t14c"), b("h14"), A.add)
        fill("capb", b("capb"), BIG)
        tt("nd4 kc", "kb", b("kb"), b("nd4"), b("kc"), A.add)
        fill("s2z", b("s2"), LOW)
        cp("t14b", "li", b("li"), b("t14b"))
        cp("t14d", "lk", b("lk"), b("t14d"))
        fill("capb", b("capb", 0, 30, 15), -BIG)
        fill("key0", b("key", 0, 1), 0.0)
        fill("capz", b("capz", 0, 112, 14), FLOOR)

    rid, pid = topo.addr(nxt)[:2]
    mask = topo.mask(core, nxt)
    engines = len(topo.engines(core, nxt))

    for r in range(ROUNDS):
        ft, fz = "ft%d" % r, "ft%d fz%d" % (r, r)
        if r:
            begin(r, T["ft%d" % (r - 1)], "ft%d" % (r - 1), "ft%d" % (r - 1))
            decode(r)
            differences()
        cp("pq0", "ps2", b("ps", 320, 448), bank(2, 128))
        tt("ps0 ps1 ps2 nd16 mask", "smk", b("smk"), T.ps[:, 0:448].indirect(b("nd16")), b("mask"), A.min)
        if r == 0:
            late_constants()
        scan("capf smk", "pmf", b("pmf"), b("capf"), b("smk"), 0.0, A.min, A.max)
        choose(0, "pmf", lambda h: (b("pmf", 224 * h + 15, 224 * h + 224, 16), b("pmf", 224 * h + 223, 224 * h + 224)),
               [scores, differences if r == 0 else nothing, nothing])
        ts("rf0", "pen", b("pen"), rows(0), 0.0, A.not_equal, -BIG, A.mult)
        turned(0, 0)
        for h in range(2):
            tt("scn pen s2z", "+s2", b("s2", 15 * h, 15 * h + 14), b("scn", 224 * h + 15, 224 * h + 224, 16), b("pen", 14 * h, 14 * h + 14), A.add)
        turned(0, 1)
        scan("capb s2 s2z", "pm1", b("pm1"), b("capb"), b("s2"), 0.0, A.min, A.max)
        tt("rf0", "+ow", b("ow", 0, 2), b("rf", 14, 495, 480), b("rf", 30, 511, 480), A.add)
        choose(1, "pm1", lambda h: (b("pm1", 15 * h, 15 * h + 14), b("pm1", 15 * h + 14, 15 * h + 15)),
               [lambda: tt("kb rf0", "+key", b("key", 1, 29), b("kb"), rows(0), A.add),
                lambda: tt("kb rf0", "+key", b("key", 57, 85), b("kb"), rows(0), A.subtract), nothing])
        column(0)
        tt("kb rf1", "+key", b("key", 29, 57), b("kb"), rows(1), A.add)
        tt("kb rf1", "+key", b("key", 85, 113), b("kb"), rows(1), A.subtract)
        tt("rf1", "+ow", b("ow", 2, 4), b("rf", 526, 1007, 480), b("rf", 542, 1023, 480), A.add)
        scan("key key0 capz", "ep", b("ep"), b("key", 0, 112), b("capz"), BIG, A.max, A.min)
        slot(0)
        tt("ep key", "tmn", b("tmn"), b("ep"), b("key", 1, 113), A.min)
        tt("ep key", "+oi", b("oi", 0, 8), b("ep", 13, 112, 14), b("key", 14, 113, 14), A.max)
        scan("capz tmn", "p2", b("p2"), b("capz"), b("tmn"), FLOOR, A.min, A.max)
        slot(1)
        cp("p2", "+oi", b("oi", 8, 16), b("p2", 13, 112, 14))
        slot(2)
        ts("oi", "oim", b("oim"), b("oi"), 2047, A.bitwise_and)
        slot(3)
        for t in range(4):
            ts("oim", "off%d" % t, b("off", 16 * t, 16 * t + 16), b("oim"), t, A.add)
        column(1)
        turned(1, 0)
        ts("av0", "av1", b("av", 0, 64), b("av", 64, 128), -1.0 / UNIT, A.mult, 0.0, A.max)
        for t in range(4):
            act(fz + " off%d" % t, "ag%d" % t, b("ag", t, 512, 4), T[ft][:, 0:XW].indirect(b("off", 16 * t, 16 * t + 8)))
        for t in range(4):
            act(fz + " ox", "+own", b("ys", 2 * t + 1, 512, 8), T[ft][:, 0:XW].indirect(b("ox", 4 * t, 4 * t + 4)), -2.0)
        for t in (2, 3, 0, 1):
            act("av%d li" % (0 if t > 1 else 1), "xg%d" % t, b("xg", 224 * t, 224 * t + 224), T.av[:, 32 * t:32 * t + 32].indirect(b("li")))
        for t in range(4):
            tt(fz + " off%d ag%d" % (t, t), "+su", b("su2", t, 512, 4), T[ft][:, 0:XW].indirect(b("off", 16 * t + 8, 16 * t + 16)), b("ag", t, 512, 4), A.add)
        turned(1, 1)
        tt("su", "mm", b("ys", 0, 512, 2), b("su2", 0, 256), b("su2", 256, 512), A.max)
        tt("eq", "ph0", b("ph0"), b("eq", 0, 28), b("eq", 28, 56), A.add)
        scan("yd mm own", "y2", b("ag"), b("yd"), b("ys"), 0.0, A.mult, A.add)
        ts("ph0", "av2", b("av", 128, 156), b("ph0"), -2.0, A.mult, 1.0, A.add)
        act("av2 li", "+sgp", b("sg", 1, 1344, 6), T.av[:, 128:160].indirect(b("li")), -1.0)
        act("av2 lk", "+sgp", b("sg", 2, 1344, 6), T.av[:, 128:160].indirect(b("lk")))
        ts("y2", "yt ag0 ag1 ag2 ag3", b("yt", 0, 256), b("ag", 1, 512, 2), 0.5, A.mult)
        quant("yt", "qy%d" % r, T["qy%d" % r][:, 0:128], T["sqy%d" % r][:, 0:128], b("yt"))
        order("g", ["qy%d" % r], [], False)
        if r == 0:
            g.wait_ge(T.sem["ready"], len(topo.engines(nxt, core)))
        arr, at = "arr%d" % r, 64 * (ROUNDS - 1 - r)
        g.remote_dma(T.ld[:, at:at + 64].bitcast(dt.uint8), T["qy%d" % r][:, 0:64].bitcast(dt.uint8), T.sem[arr], T.sem["loc"], pid, rid, mask)
        g.remote_dma(T.sld[:, at:at + 64], T["sqy%d" % r][:, 0:64], T.sem[arr], T.sem["loc"], pid, rid, mask)
        nloc[0] += 2 * engines
        for t in (2, 3, 0, 1):
            w = (64 + 32 * t) % 128
            tt("av0 av1 lk xg%d" % t, "+pr", b("st", 2 + t, 1344, 6), T.av[:, w:w + 32].indirect(b("lk")), b("xg", 224 * t, 224 * t + 224), A.mult)
        act("yt", "y32", b("y32"), b("yt", 0, 256), 32.0)
        scan("sgc sgp st1 cst pr", "so", b("so"), b("sg"), b("st"), 0.0, A.mult, A.add)
        ts("so", "cst", b("st", 0, 1344, 6), b("so", 5, 1344, 6), 3 * UNIT, A.min, -3 * UNIT, A.max)
        if r == 0:
            quant("vt", "qv", b("qv"), b("sqv"), b("vt"))
        if r == ROUNDS - 1:
            fill("cwk", b("cw", 512, 513), 0.0)
            tt("oe0 lane", "oe", b("oe"), b("oe0"), b("lane", 0, 25), A.add)
            ts("oe", "o1", b("o1"), b("oe"), -6.5, A.add, 1.0 / 14.0, A.mult)
            ts("o1", "o2", b("o2"), b("o1"), RND0, A.add, RND0, A.subtract)
            ts("o2", "o3", b("o3"), b("o2"), 2.0, A.mult, 32.5, A.add)
            tt("o3 oe", "o4", b("o4"), b("o3"), b("oe"), A.add)
            ts("o4", "loa", b("loa"), b("o4"), 2.0, A.mult)
        stored()
        lay_out()
        if r == ROUNDS - 1:
            act("ds1 loa", "oa1", b("oa1"), T.ds1[:, 0:1024].indirect(b("loa")), 1.0 / UNIT)
            dma("y", "oa1", "", T.oa[:, :], b("oa1", 0, 392))
        order("t", [], ["land%d" % r], False)
        entry("land%d" % r)[0].append((arr, 2 * len(topo.engines(prv, core)), "remote"))
        toks = ("pq0", "pq1", "pp0", "pp1")

        def place(k, cols):
            return T.pq[:, 512 * k:512 * k + cols] if k < 2 else T.pp[:, 512 * (k - 2):512 * (k - 2) + cols]

        def sum_(k):
            tt(toks[k] + " y32", "+wb%d" % (k // 2), b("wb", 64 * k, 64 * k + 64), place(k, 64), b("y32", k, 256, 4), A.add)

        def scaled(k):
            ts("wb%d" % k, "vv%d" % k, b("vv", 128 * k, 128 * k + 128), b("wb", 128 * k, 128 * k + 128), 0.03125, A.mult)

        def scatter(k):
            cp("vv%d ox" % k, ft, T[ft][:, 0:XW].indirect(b("ox", 8 * k, 8 * k + 8)), b("vv", 128 * k, 128 * k + 128))

        for k in range(4):
            mm("qw sw ldz land%d" % r, toks[k], place(k, 128), T.qw[:, 128 * k:128 * k + 128], T.sqw[:, 128 * k:128 * k + 128],
               b("ld", at, at + 128), b("sld", at, at + 128))
        sum_(0)
        sum_(1)
        sum_(2)
        scaled(0)
        sum_(3)
        scatter(0)
        scaled(1)
        scatter(1)
    qx, sx = quantise_state(3, T[ft], ft, ft)
    for k in range(3):
        lo, hi = CUTS[k], CUTS[k + 1]
        mm("qv q%d3" % k, ("pp0", "pp1", "pq0")[k], bank(k, hi - lo), b("qv"), b("sqv"), qx[:, lo:hi], sx[:, lo:hi])
    act("pp0", "yo0", b("yo", 0, 160), bank(0, 160))
    act("pp1", "yo1", b("yo", 160, 320), bank(1, 160))
    cp("pq0", "yo2", b("yo", 320, 448), bank(2, 128))
    dma("y", "q03 q13", "", T.oc[:, 0:1280], qx[:, 0:320].bitcast(dt.uint8))
    dma("s", "yo0 yo1", "", T.y[:, 0:320], b("yo", 0, 320))
    dma("y", "yo2", "", T.y[:, 320:448], b("yo", 320, 448))
    dma("s", "q23", "", T.oc[:, 1280:1792], qx[:, 320:448].bitcast(dt.uint8))
    for k in range(4):
        dma("sy"[k % 2], "q03 q13 q23", "", T.osc[4 * k:4 * k + 4, 0:448], sx[32 * k:32 * k + 4, 0:448])
    g.wait_ge(T.sem["loc"], nloc[0])
    for k in range(ndma[0]):
        need("y", "dma%d" % k, 16)
    for s in ("cv", "cs", "ct", "cg"):
        need("y", s, count[s])
